import numpy as np
import ml_dtypes


def mxq(x, axis, fmt="e4m3"):
    dtype, down = {"e4m3": (ml_dtypes.float8_e4m3fn, 7), "e5m2": (ml_dtypes.float8_e5m2, 14)}[fmt]
    v = np.moveaxis(np.asarray(x, np.float32).astype(ml_dtypes.bfloat16).astype(np.float64), axis, -1)
    blocks = v.reshape(v.shape[:-1] + (-1, 32))
    amax = np.abs(blocks).max(-1, keepdims=True)
    byte = np.maximum(np.where(amax > 0, np.frexp(amax)[1] - 1 + 127, 0) - down, 1)
    scale = np.exp2(byte - 127.0)
    codes = (blocks / scale).astype(np.float32).astype(dtype).astype(np.float64)
    return np.moveaxis((codes * scale).reshape(v.shape), -1, axis)


WIDE = False


def mx_kscale(k):
    if not WIDE:
        return np.ones(k)
    levels = np.array([10, -10, 5, -5, 0])
    if k % 512:
        return np.exp2(np.random.permutation(np.resize(levels, k // 32))).repeat(32)
    a = np.empty((k // 512, 16))
    for p in range(k // 512):
        a[p, :8] = np.random.permutation(np.resize(levels, 8))
        for g in range(8):
            far = levels[np.abs(levels - a[p, g]) >= 10]
            a[p, g + 8] = far[np.random.randint(len(far))]
    return np.exp2(a.ravel()).repeat(32)


def f64(x):
    return np.asarray(x).astype(np.float64)


def striped(idx):
    return np.tile(np.asarray(idx).reshape(-1, 16).T, (8, 1)).astype(np.uint16)


def unstriped(offs):
    return offs[:16].T.reshape(-1).astype(np.int64)


E2M1 = np.array([0.0, 0.5, 1.0, 1.5, 2.0, 3.0, 4.0, 6.0, -0.0, -0.5, -1.0, -1.5, -2.0, -3.0, -4.0, -6.0])


def pack_weight(w, fmt):
    k, n = w.shape
    w = f64(np.asarray(w, np.float32).astype(ml_dtypes.bfloat16)).reshape(k // 32, 32, n)
    amax = np.abs(w).max(1)
    if fmt == "e4m3":
        byte = np.frexp(amax)[1] - 1 + 127 - 7
    else:
        mant, ex = np.frexp(amax / 6.0)
        byte = np.where(mant > 0.5, ex, ex - 1) + 127
    byte = np.clip(np.where(amax > 0, byte, 1), 1, 254)
    scaled = (w * np.exp2(127.0 - byte)[:, None, :]).reshape(k, n).astype(np.float32)
    by_word = np.ascontiguousarray(scaled.reshape(k // 512, 128, 4, n).transpose(0, 1, 3, 2))
    if fmt == "e4m3":
        words = by_word.astype(ml_dtypes.float8_e4m3fn).view(np.uint8)
    else:
        c = by_word.astype(ml_dtypes.float4_e2m1fn).view(np.uint8) & 0xF
        words = (c[..., 0::2] | (c[..., 1::2] << 4)).reshape(k // 512, 128, 2 * n)
    return np.ascontiguousarray(words), np.ascontiguousarray(byte.astype(np.uint8).reshape(k // 512, 16, n))


def unpack_weight(words, scales, fmt):
    g, _, n = scales.shape
    words = np.ascontiguousarray(words).reshape(g, 128, n, -1)
    if fmt == "e4m3":
        vals = words.view(ml_dtypes.float8_e4m3fn).astype(np.float64)
    else:
        nib = np.empty((g, 128, n, 4), np.uint8)
        nib[..., 0::2] = words & 0xF
        nib[..., 1::2] = words >> 4
        vals = E2M1[nib]
    vals = vals * np.repeat(np.exp2(scales.astype(np.float64) - 127.0), 8, axis=1)[..., None]
    return vals.transpose(0, 1, 3, 2).reshape(g * 512, n)


def sigmoid(v):
    return 1.0 / (1.0 + np.exp(-v))


def bf(x):
    return np.asarray(x, np.float32).astype(ml_dtypes.bfloat16)


def planes(Y):
    r, m = Y.shape
    b = f64(bf(Y)).reshape(r // 32, 32, m)
    amax = np.abs(b).max(1)
    byte = np.clip(np.where(amax > 0, np.frexp(amax)[1] - 1 + 127 - 7, 1), 1, 254)
    codes = (b * np.exp2(127.0 - byte)[:, None, :]).reshape(r, m).astype(np.float32).astype(ml_dtypes.float8_e4m3fn).view(np.uint8)
    words = codes.reshape(r // 512, 128, 4, m).transpose(0, 1, 3, 2)
    return np.ascontiguousarray(words), np.ascontiguousarray(byte.astype(np.uint8).reshape(r // 512, 16, m))


B, N, T, D, NQ = 1, 512, 2048, 1024, 512


def setup_inputs():
    n = np.random.standard_normal
    idx = np.random.permutation(T)[:B * N]
    s = mx_kscale(D)[:, None]
    kp = pack_weight(n((D, T)) / s, "e4m3")
    cp = pack_weight(n((D, T)) / s, "e2m1")
    return {
        "qT": (n((B, D, NQ)) * s * (1.00 / np.sqrt(D))).astype(np.float32),
        "k_words": kp[0],
        "k_scales": kp[1],
        "c_words": np.ascontiguousarray(cp[0].reshape(1, 2, 128, T, 2).transpose(0, 2, 3, 1, 4)).reshape(1, 128, T, 4),
        "c_scales": cp[1],
        "th": (n((B, 1, NQ)) + 1).astype(np.float32),
        "offs": striped(idx),
    }


def reference(qT, k_words, k_scales, c_words, c_scales, th, offs):
    idx = unstriped(offs)
    pick = lambda x, which: x[:, which].reshape(x.shape[0], B, -1).transpose(1, 0, 2)
    k = unpack_weight(k_words, k_scales, "e4m3")
    kg = pick(k, idx)
    c = unpack_weight(c_words.reshape(1, 128, T, 2, 2).transpose(0, 3, 1, 2, 4).reshape(2, 128, 2 * T), c_scales, "e2m1")
    cg = pick(c, idx)
    qq = mxq(f64(qT), 1, "e4m3")
    a = kg.transpose(0, 2, 1) @ qq
    z = cg.transpose(0, 2, 1) @ qq
    y = sigmoid(np.maximum(a, z) - f64(th))
    Y = y[0]
    words, scales = planes(Y)
    return Y, words, scales

@@ -1,0 +1,210 @@
+from contextlib import ExitStack
+
+import concourse.mybir as mybir
+from concourse.masks import make_identity
+
+F32 = mybir.dt.float32
+BF16 = mybir.dt.bfloat16
+I32 = mybir.dt.int32
+U32 = mybir.dt.uint32
+U16 = mybir.dt.uint16
+U8 = mybir.dt.uint8
+FP8X4 = mybir.dt.float8_e4m3fn_x4
+FP4X4 = mybir.dt.float4_e2m1fn_x4
+ALU = mybir.AluOpType
+ACT = mybir.ActivationFunctionType
+
+P = 128
+PACK = 4
+SLOTS, TOKENS, FEATURES, QUERIES = 512, 2048, 1024, 512
+PASSES = FEATURES // (P * PACK)
+CHUNKS = QUERIES // P
+HALF = QUERIES // 2
+FLOPS = 2 * 2 * SLOTS * FEATURES * QUERIES
+
+
+def tile_attend_plw_proto_topk_kernel(tc, qT, k_words, k_scales, c_words, c_scales, th, offs, out_0, out_1, out_2):
+    nc = tc.nc
+    with ExitStack() as ctx:
+        keep = ctx.enter_context(tc.tile_pool(name="keep", bufs=1))
+        a_psum = ctx.enter_context(tc.psum_pool(name="a_psum", bufs=4))
+        z_psum = ctx.enter_context(tc.psum_pool(name="z_psum", bufs=4))
+
+        def held(shape, dtype, name, tag=None):
+            return keep.tile(shape, dtype, name=name, tag=tag or name, align_bytes=64)
+
+        offsets = held([P, SLOTS // 16], U16, "offsets")
+        c_pool = held([P, TOKENS], U32, "c_pool", "first_pool")
+        c_scale_pool = held([P, PASSES, TOKENS], U8, "c_scale_pool", "third_pool")
+        k_scale_pool = held([P, TOKENS], U8, "k_scale_pool")
+        th_rows = held([P, P], F32, "th_rows")
+        identity = held([P, P], F32, "identity")
+        warm = held([P, 16], F32, "warm")
+        q_raw = [held([P, PACK, QUERIES], F32, "q_raw0")]
+
+        def load_queries(o):
+            nc.sync.dma_start(q_raw[o][:], qT[0, 512 * o : 512 * (o + 1), :].rearrange("(p j) w -> p j w", j=PACK))
+
+        nc.vector.memset(c_scale_pool[:].rearrange("p o t -> p (o t)").bitcast(I32), 0)
+        nc.vector.memset(warm[:, 0:1], 0.0)
+        nc.gpsimd.memset(th_rows[:], 0.0)
+        make_identity(nc, identity[:])
+        nc.vector.memset(k_scale_pool[:].bitcast(I32), 0)
+
+        nc.sync.dma_start(offsets[:], offs)
+        nc.sync.dma_start(c_pool[:].bitcast(I32), c_words[0].rearrange("p t b -> p (t b)").bitcast(I32))
+        load_queries(0)
+        nc.scalar.dma_start(th_rows[0:CHUNKS, :], th[0, 0].rearrange("(j p) -> j p", p=P))
+        for quad in range(4):
+            nc.scalar.dma_start(
+                c_scale_pool[32 * quad : 32 * quad + 4].bitcast(I32),
+                c_scales[:, 4 * quad : 4 * quad + 4, :].rearrange("o r t -> r o t").bitcast(I32),
+            )
+        nc.scalar.activation(out=warm[:, 8:9], in_=warm[:, 0:1], func=ACT.Sigmoid)
+        for quad in range(4):
+            nc.scalar.dma_start(
+                k_scale_pool[32 * quad + 4 : 32 * quad + 12, :].bitcast(I32),
+                k_scales[:, 4 * quad : 4 * quad + 4, :].bitcast(I32),
+            )
+
+        th_turned = z_psum.tile([P, P], F32, name="th_turned", tag="z")
+        nc.tensor.transpose(th_turned[:], th_rows[:], identity[:])
+        minus_th = held([P, CHUNKS], F32, "minus_th")
+        nc.vector.tensor_scalar(out=minus_th[:], in0=th_turned[:, 0:CHUNKS], scalar1=-1.0, scalar2=None, op0=ALU.mult)
+
+        c_listed = held([P, SLOTS], U32, "c_listed", "second_pool")
+        nc.vector.tensor_copy(c_listed[:], c_pool[:].indirect(offsets[:]))
+        q_raw.append(held([P, PACK, QUERIES], F32, "q_raw1", "first_pool"))
+        load_queries(1)
+        c_codes = [held([P, 2 * SLOTS], U8, "c_codes%d" % o) for o in range(PASSES)]
+        c_halves = c_listed[:].bitcast(U16).rearrange("p (n h) -> p h n", h=2)
+        for o in range(PASSES):
+            nc.vector.tensor_copy(c_codes[o][:].bitcast(U16), c_halves[:, o, :])
+        k_pool = []
+
+        def load_first_keys(o, tag):
+            k_pool.append(held([P, TOKENS], U32, "k_pool%d" % o, tag))
+            nc.sync.dma_start(k_pool[o][:].bitcast(I32), k_words[o].rearrange("p t b -> p (t b)").bitcast(I32))
+
+        load_first_keys(0, "second_pool")
+        c_scale = [held([P, SLOTS], U8, "c_scale%d" % o) for o in range(PASSES)]
+        for o in range(PASSES):
+            nc.vector.tensor_copy(c_scale[o][:], c_scale_pool[:, o, :].indirect(offsets[:]))
+        load_first_keys(1, "third_pool")
+        k_scale = held([P, SLOTS], U8, "k_scale")
+        nc.vector.tensor_copy(k_scale[:], k_scale_pool[:].indirect(offsets[:]))
+
+        q_codes = {}
+        q_scale = {}
+
+        def round_queries(o, h, copy):
+            grouped = held([P, HALF, PACK], BF16, "q_grouped%d%d" % (o, h))
+            copy(
+                grouped[:].rearrange("p (c i) t -> p c t i", i=4),
+                q_raw[o][:, :, h * HALF : (h + 1) * HALF].rearrange("p t (c i) -> p c t i", i=4),
+            )
+            return grouped
+
+        def quantize_queries(o, h, grouped):
+            q_codes[o, h] = held([P, HALF], U32, "q_codes%d%d" % (o, h))
+            q_scale[o, h] = held([P, HALF], U8, "q_scale%d%d" % (o, h))
+            nc.vector.quantize_mx(
+                out=q_codes[o, h][:].bitcast(FP8X4), scales=q_scale[o, h][:], in_=grouped[:].rearrange("p w t -> p (w t)")
+            )
+
+        def scores(bank, j, o, codes, scale):
+            h, cols = j // 2, slice((j % 2) * P, (j % 2 + 1) * P)
+            nc.tensor.matmul_mx(
+                out=bank[:],
+                lhsT=q_codes[o, h][:, cols].bitcast(FP8X4),
+                lhsT_scale=q_scale[o, h][:, cols],
+                rhs=codes,
+                rhs_scale=scale,
+                start=(o == 0),
+                stop=(o == PASSES - 1),
+            )
+
+        g00 = round_queries(0, 0, nc.scalar.copy)
+        g01 = round_queries(0, 1, nc.scalar.copy)
+        quantize_queries(0, 0, g00)
+        g10 = round_queries(1, 0, nc.vector.tensor_copy)
+        quantize_queries(0, 1, g01)
+        g11 = round_queries(1, 1, nc.scalar.copy)
+        quantize_queries(1, 0, g10)
+
+        k_codes = [held([P, SLOTS], U32, "k_codes%d" % o) for o in range(PASSES)]
+        z_less_th = []
+
+        def second_scores(j):
+            z_bank = z_psum.tile([P, SLOTS], F32, name="z_bank", tag="z")
+            for o in range(PASSES):
+                scores(z_bank, j, o, c_codes[o][:].bitcast(FP4X4), c_scale[o][:])
+            dealt = held([P, PACK, P], F32, "z_less_th%d" % j)
+            nc.scalar.activation(
+                out=dealt[:],
+                in_=z_bank[:].rearrange("p (s r) -> p r s", r=PACK),
+                func=ACT.Identity,
+                bias=minus_th[:, j : j + 1],
+            )
+            z_less_th.append(dealt)
+
+        second_scores(0)
+        second_scores(1)
+        nc.vector.tensor_copy(k_codes[0][:], k_pool[0][:].indirect(offsets[:]))
+        quantize_queries(1, 1, g11)
+        second_scores(2)
+        second_scores(3)
+
+        a_banks = [a_psum.tile([P, SLOTS], F32, name="a_bank", tag="a") for j in range(CHUNKS)]
+        for j in range(CHUNKS):
+            scores(a_banks[j], j, 0, k_codes[0][:].bitcast(FP8X4), k_scale[4:P, :])
+        nc.vector.tensor_copy(k_codes[1][:], k_pool[1][:].indirect(offsets[:]))
+        for j in range(CHUNKS):
+            scores(a_banks[j], j, 1, k_codes[1][:].bitcast(FP8X4), k_scale[8:P, :])
+
+        y_codes = held([P, QUERIES], U32, "y_codes")
+        y_scale = held([P, QUERIES], U8, "y_scale")
+        y_rows = out_0.rearrange("(p r) q -> p r q", r=PACK)
+        word_rows = out_1[0].rearrange("p q b -> p (q b)").bitcast(I32)
+        weights = {}
+
+        def weigh(j):
+            best = held([P, PACK, P], F32, "best%d" % j)
+            nc.vector.scalar_tensor_tensor(
+                out=best[:],
+                in0=a_banks[j][:].rearrange("p (s r) -> p r s", r=PACK),
+                scalar=minus_th[:, j : j + 1],
+                in1=z_less_th[j][:],
+                op0=ALU.add,
+                op1=ALU.max,
+            )
+            turned = z_psum.tile([P, PACK, P], F32, name="turned", tag="z")
+            for r in range(PACK):
+                nc.tensor.transpose(turned[:, r, :], best[:, r, :], identity[:])
+            weights[j] = held([P, PACK, P], F32, "weights%d" % j)
+            nc.scalar.activation(out=weights[j][:], in_=turned[:], func=ACT.Sigmoid)
+            nc.sync.dma_start(y_rows[:, :, j * P : (j + 1) * P], weights[j][:])
+
+        def hand_on(j):
+            cols = slice(j * P, (j + 1) * P)
+            grouped = held([P, P, PACK], BF16, "y_grouped%d" % j)
+            nc.vector.tensor_copy(
+                grouped[:].rearrange("p (c i) r -> p c r i", i=4),
+                weights[j][:].rearrange("p r (c i) -> p c r i", i=4),
+            )
+            nc.vector.quantize_mx(
+                out=y_codes[:, cols].bitcast(FP8X4), scales=y_scale[:, cols], in_=grouped[:].rearrange("p q r -> p (q r)")
+            )
+            if j % 2 == 1:
+                pair = slice((j - 1) * P, (j + 1) * P)
+                nc.sync.dma_start(word_rows[:, pair], y_codes[:, pair].bitcast(I32))
+
+        for j in range(CHUNKS):
+            weigh(j)
+        for j in range(CHUNKS):
+            hand_on(j)
+        for quad in range(4):
+            queue = nc.scalar if quad % 2 == 0 else nc.sync
+            queue.dma_start(
+                out_2[0, 4 * quad : 4 * quad + 4, :].bitcast(I32), y_scale[32 * quad : 32 * quad + 4, :].bitcast(I32)
+            )

@@ -35,132 +35,146 @@ def tile_attend_plw_proto_topk_kernel(tc, qT, k_words, k_scales, c_words, c_scal
 
         offsets = held([P, SLOTS // 16], U16, "offsets")
         c_pool = held([P, TOKENS], U32, "c_pool", "first_pool")
-        c_scale_pool = held([P, PASSES, TOKENS], U8, "c_scale_pool", "third_pool")
-        k_scale_pool = held([P, TOKENS], U8, "k_scale_pool")
+        c_scale_pool = held([P, TOKENS], U8, "c_scale_pool")
+        k_scale_pool = held([P, TOKENS], U8, "k_scale_pool", "third_pool")
+        c_scale = held([P, PASSES, SLOTS], U8, "c_scale")
+        k_scale = held([P, PASSES, SLOTS], U8, "k_scale")
         th_rows = held([P, P], F32, "th_rows")
         identity = held([P, P], F32, "identity")
         warm = held([P, 16], F32, "warm")
-        q_raw = [held([P, PACK, QUERIES], F32, "q_raw0")]
 
-        def load_queries(o):
-            nc.sync.dma_start(q_raw[o][:], qT[0, 512 * o : 512 * (o + 1), :].rearrange("(p j) w -> p j w", j=PACK))
+        def load_queries(o, first, chunks, tag):
+            raw = held([P, PACK, chunks * P], F32, "q_raw%d%d" % (o, first), tag)
+            rows = qT[0, 512 * o : 512 * (o + 1), first * P : (first + chunks) * P]
+            nc.sync.dma_start(raw[:], rows.rearrange("(p j) w -> p j w", j=PACK))
+            return raw
 
-        nc.vector.memset(c_scale_pool[:].rearrange("p o t -> p (o t)").bitcast(I32), 0)
         nc.vector.memset(warm[:, 0:1], 0.0)
+        for pool in (c_scale_pool, k_scale_pool):
+            nc.vector.memset(pool[0:96, :].bitcast(I32), 0)
+        for plane in (c_scale, k_scale):
+            nc.vector.memset(plane[:].rearrange("p o n -> p (o n)").bitcast(I32), 0)
         nc.gpsimd.memset(th_rows[:], 0.0)
         make_identity(nc, identity[:])
-        nc.vector.memset(k_scale_pool[:].bitcast(I32), 0)
 
         nc.sync.dma_start(offsets[:], offs)
+        for pool, scales in ((c_scale_pool, c_scales), (k_scale_pool, k_scales)):
+            nc.sync.dma_start(pool[96:P, :].bitcast(I32), scales.rearrange("o f t -> f o t").bitcast(I32))
         nc.sync.dma_start(c_pool[:].bitcast(I32), c_words[0].rearrange("p t b -> p (t b)").bitcast(I32))
-        load_queries(0)
+        q_first = load_queries(0, 0, CHUNKS, "first_queries")
         nc.scalar.dma_start(th_rows[0:CHUNKS, :], th[0, 0].rearrange("(j p) -> j p", p=P))
-        for quad in range(4):
-            nc.scalar.dma_start(
-                c_scale_pool[32 * quad : 32 * quad + 4].bitcast(I32),
-                c_scales[:, 4 * quad : 4 * quad + 4, :].rearrange("o r t -> r o t").bitcast(I32),
-            )
         nc.scalar.activation(out=warm[:, 8:9], in_=warm[:, 0:1], func=ACT.Sigmoid)
-        for quad in range(4):
-            nc.scalar.dma_start(
-                k_scale_pool[32 * quad + 4 : 32 * quad + 12, :].bitcast(I32),
-                k_scales[:, 4 * quad : 4 * quad + 4, :].bitcast(I32),
-            )
 
-        th_turned = z_psum.tile([P, P], F32, name="th_turned", tag="z")
-        nc.tensor.transpose(th_turned[:], th_rows[:], identity[:])
-        minus_th = held([P, CHUNKS], F32, "minus_th")
-        nc.vector.tensor_scalar(out=minus_th[:], in0=th_turned[:, 0:CHUNKS], scalar1=-1.0, scalar2=None, op0=ALU.mult)
+        def gather_scales(pool, plane, name):
+            listed = held([P, SLOTS], U8, name)
+            nc.vector.tensor_copy(listed[:], pool[:].indirect(offsets[:]))
+            for quad in range(4):
+                nc.scalar.dma_start(
+                    plane[32 * quad : 32 * quad + 4].bitcast(I32),
+                    listed[96 + 8 * quad : 96 + 8 * quad + 8, :].bitcast(I32),
+                )
 
-        c_listed = held([P, SLOTS], U32, "c_listed", "second_pool")
-        nc.vector.tensor_copy(c_listed[:], c_pool[:].indirect(offsets[:]))
-        q_raw.append(held([P, PACK, QUERIES], F32, "q_raw1", "first_pool"))
-        load_queries(1)
-        c_codes = [held([P, 2 * SLOTS], U8, "c_codes%d" % o) for o in range(PASSES)]
-        c_halves = c_listed[:].bitcast(U16).rearrange("p (n h) -> p h n", h=2)
-        for o in range(PASSES):
-            nc.vector.tensor_copy(c_codes[o][:].bitcast(U16), c_halves[:, o, :])
+        gather_scales(c_scale_pool, c_scale, "c_scale_listed")
+        gather_scales(k_scale_pool, k_scale, "k_scale_listed")
+        q_second = load_queries(1, 0, CHUNKS - 1, "third_pool")
+
         k_pool = []
 
         def load_first_keys(o, tag):
             k_pool.append(held([P, TOKENS], U32, "k_pool%d" % o, tag))
             nc.sync.dma_start(k_pool[o][:].bitcast(I32), k_words[o].rearrange("p t b -> p (t b)").bitcast(I32))
 
-        load_first_keys(0, "second_pool")
-        c_scale = [held([P, SLOTS], U8, "c_scale%d" % o) for o in range(PASSES)]
+        c_listed = held([P, SLOTS], U32, "c_listed", "second_pool")
+        nc.vector.tensor_copy(c_listed[:], c_pool[:].indirect(offsets[:]))
+        load_first_keys(0, "first_pool")
+        c_codes = [held([P, 2 * SLOTS], U8, "c_codes%d" % o) for o in range(PASSES)]
+        c_halves = c_listed[:].bitcast(U16).rearrange("p (n h) -> p h n", h=2)
         for o in range(PASSES):
-            nc.vector.tensor_copy(c_scale[o][:], c_scale_pool[:, o, :].indirect(offsets[:]))
-        load_first_keys(1, "third_pool")
-        k_scale = held([P, SLOTS], U8, "k_scale")
-        nc.vector.tensor_copy(k_scale[:], k_scale_pool[:].indirect(offsets[:]))
+            nc.vector.tensor_copy(c_codes[o][:].bitcast(U16), c_halves[:, o, :])
+        load_first_keys(1, "second_pool")
+
+        th_turned = z_psum.tile([P, P], F32, name="th_turned", tag="z")
+        nc.tensor.transpose(th_turned[:], th_rows[:], identity[:])
+        minus_th = held([P, CHUNKS], F32, "minus_th")
+        nc.vector.tensor_scalar(out=minus_th[:], in0=th_turned[:, 0:CHUNKS], scalar1=-1.0, scalar2=None, op0=ALU.mult)
 
         q_codes = {}
         q_scale = {}
 
-        def round_queries(o, h, copy):
-            grouped = held([P, HALF, PACK], BF16, "q_grouped%d%d" % (o, h))
+        def round_queries(o, first, chunks, raw, copy):
+            grouped = held([P, chunks * P, PACK], BF16, "q_grouped%d%d" % (o, first))
             copy(
                 grouped[:].rearrange("p (c i) t -> p c t i", i=4),
-                q_raw[o][:, :, h * HALF : (h + 1) * HALF].rearrange("p t (c i) -> p c t i", i=4),
+                raw.rearrange("p t (c i) -> p c t i", i=4),
             )
-            return grouped
+            return o, first, chunks, grouped
 
-        def quantize_queries(o, h, grouped):
-            q_codes[o, h] = held([P, HALF], U32, "q_codes%d%d" % (o, h))
-            q_scale[o, h] = held([P, HALF], U8, "q_scale%d%d" % (o, h))
+        def quantize_queries(o, first, chunks, grouped):
+            codes = held([P, chunks * P], U32, "q_codes%d%d" % (o, first))
+            scale = held([P, chunks * P], U8, "q_scale%d%d" % (o, first))
             nc.vector.quantize_mx(
-                out=q_codes[o, h][:].bitcast(FP8X4), scales=q_scale[o, h][:], in_=grouped[:].rearrange("p w t -> p (w t)")
+                out=codes[:].bitcast(FP8X4), scales=scale[:], in_=grouped[:].rearrange("p w t -> p (w t)")
             )
+            for c in range(chunks):
+                q_codes[o, first + c] = codes[:, c * P : (c + 1) * P]
+                q_scale[o, first + c] = scale[:, c * P : (c + 1) * P]
 
         def scores(bank, j, o, codes, scale):
-            h, cols = j // 2, slice((j % 2) * P, (j % 2 + 1) * P)
             nc.tensor.matmul_mx(
                 out=bank[:],
-                lhsT=q_codes[o, h][:, cols].bitcast(FP8X4),
-                lhsT_scale=q_scale[o, h][:, cols],
+                lhsT=q_codes[o, j].bitcast(FP8X4),
+                lhsT_scale=q_scale[o, j],
                 rhs=codes,
                 rhs_scale=scale,
                 start=(o == 0),
                 stop=(o == PASSES - 1),
             )
 
-        g00 = round_queries(0, 0, nc.scalar.copy)
-        g01 = round_queries(0, 1, nc.scalar.copy)
-        quantize_queries(0, 0, g00)
-        g10 = round_queries(1, 0, nc.vector.tensor_copy)
-        quantize_queries(0, 1, g01)
-        g11 = round_queries(1, 1, nc.scalar.copy)
-        quantize_queries(1, 0, g10)
+        g00 = round_queries(0, 0, 2, q_first[:, :, 0:HALF], nc.scalar.copy)
+        g02 = round_queries(0, 2, 2, q_first[:, :, HALF:QUERIES], nc.scalar.copy)
+        q_last = load_queries(1, CHUNKS - 1, 1, "first_queries")
+        quantize_queries(*g00)
+        g10 = round_queries(1, 0, 2, q_second[:, :, 0:HALF], nc.vector.tensor_copy)
+        quantize_queries(*g02)
+        g12 = round_queries(1, 2, 1, q_second[:, :, HALF : HALF + P], nc.scalar.copy)
+        quantize_queries(*g10)
 
         k_codes = [held([P, SLOTS], U32, "k_codes%d" % o) for o in range(PASSES)]
-        z_less_th = []
+        z_banks = [z_psum.tile([P, SLOTS], F32, name="z_bank", tag="z") for j in range(CHUNKS)]
+        a_banks = [a_psum.tile([P, SLOTS], F32, name="a_bank", tag="a") for j in range(CHUNKS)]
+        z_less_th = {}
 
-        def second_scores(j):
-            z_bank = z_psum.tile([P, SLOTS], F32, name="z_bank", tag="z")
-            for o in range(PASSES):
-                scores(z_bank, j, o, c_codes[o][:].bitcast(FP4X4), c_scale[o][:])
-            dealt = held([P, PACK, P], F32, "z_less_th%d" % j)
+        def second_scores(j, o):
+            scores(z_banks[j], j, o, c_codes[o][:].bitcast(FP4X4), c_scale[:, o, :])
+
+        def first_scores(j, o):
+            scores(a_banks[j], j, o, k_codes[o][:].bitcast(FP8X4), k_scale[:, o, :])
+
+        def shift_second_scores(j):
+            z_less_th[j] = held([P, PACK, P], F32, "z_less_th%d" % j)
             nc.scalar.activation(
-                out=dealt[:],
-                in_=z_bank[:].rearrange("p (s r) -> p r s", r=PACK),
+                out=z_less_th[j][:],
+                in_=z_banks[j][:].rearrange("p (s r) -> p r s", r=PACK),
                 func=ACT.Identity,
                 bias=minus_th[:, j : j + 1],
             )
-            z_less_th.append(dealt)
 
-        second_scores(0)
-        second_scores(1)
+        for j in range(CHUNKS):
+            second_scores(j, 0)
+        quantize_queries(*g12)
+        for j in range(CHUNKS - 1):
+            second_scores(j, 1)
+            shift_second_scores(j)
         nc.vector.tensor_copy(k_codes[0][:], k_pool[0][:].indirect(offsets[:]))
-        quantize_queries(1, 1, g11)
-        second_scores(2)
-        second_scores(3)
-
-        a_banks = [a_psum.tile([P, SLOTS], F32, name="a_bank", tag="a") for j in range(CHUNKS)]
         for j in range(CHUNKS):
-            scores(a_banks[j], j, 0, k_codes[0][:].bitcast(FP8X4), k_scale[4:P, :])
+            first_scores(j, 0)
         nc.vector.tensor_copy(k_codes[1][:], k_pool[1][:].indirect(offsets[:]))
-        for j in range(CHUNKS):
-            scores(a_banks[j], j, 1, k_codes[1][:].bitcast(FP8X4), k_scale[8:P, :])
+        quantize_queries(*round_queries(1, CHUNKS - 1, 1, q_last[:], nc.scalar.copy))
+        for j in range(CHUNKS - 1):
+            first_scores(j, 1)
+        second_scores(CHUNKS - 1, 1)
+        shift_second_scores(CHUNKS - 1)
+        first_scores(CHUNKS - 1, 1)
 
         y_codes = held([P, QUERIES], U32, "y_codes")
         y_scale = held([P, QUERIES], U8, "y_scale")

@@ -16,10 +16,17 @@ ACT = mybir.ActivationFunctionType
 
 P = 128
 PACK = 4
+QUADRANT = 32
+QUADRANTS = P // QUADRANT
+SCALE_ROWS = 4
+LINE = 4
 SLOTS, TOKENS, FEATURES, QUERIES = 512, 2048, 1024, 512
-PASSES = FEATURES // (P * PACK)
+PASS_FEATURES = P * PACK
+PASSES = FEATURES // PASS_FEATURES
 CHUNKS = QUERIES // P
+LAST_CHUNK = CHUNKS - 1
 HALF = QUERIES // 2
+LOADED_ROWS = P - QUADRANT
 FLOPS = 2 * 2 * SLOTS * FEATURES * QUERIES
 
 
@@ -27,8 +34,8 @@ def tile_attend_plw_proto_topk_kernel(tc, qT, k_words, k_scales, c_words, c_scal
     nc = tc.nc
     with ExitStack() as ctx:
         keep = ctx.enter_context(tc.tile_pool(name="keep", bufs=1))
-        a_psum = ctx.enter_context(tc.psum_pool(name="a_psum", bufs=4))
-        z_psum = ctx.enter_context(tc.psum_pool(name="z_psum", bufs=4))
+        a_psum = ctx.enter_context(tc.psum_pool(name="a_psum", bufs=CHUNKS))
+        z_psum = ctx.enter_context(tc.psum_pool(name="z_psum", bufs=CHUNKS))
 
         def held(shape, dtype, name, tag=None):
             return keep.tile(shape, dtype, name=name, tag=tag or name, align_bytes=64)
@@ -45,13 +52,13 @@ def tile_attend_plw_proto_topk_kernel(tc, qT, k_words, k_scales, c_words, c_scal
 
         def load_queries(o, first, chunks, tag):
             raw = held([P, PACK, chunks * P], F32, "q_raw%d%d" % (o, first), tag)
-            rows = qT[0, 512 * o : 512 * (o + 1), first * P : (first + chunks) * P]
+            rows = qT[0, PASS_FEATURES * o : PASS_FEATURES * (o + 1), first * P : (first + chunks) * P]
             nc.sync.dma_start(raw[:], rows.rearrange("(p j) w -> p j w", j=PACK))
             return raw
 
         nc.vector.memset(warm[:, 0:1], 0.0)
         for pool in (c_scale_pool, k_scale_pool):
-            nc.vector.memset(pool[0:96, :].bitcast(I32), 0)
+            nc.vector.memset(pool[0:LOADED_ROWS, :].bitcast(I32), 0)
         for plane in (c_scale, k_scale):
             nc.vector.memset(plane[:].rearrange("p o n -> p (o n)").bitcast(I32), 0)
         nc.gpsimd.memset(th_rows[:], 0.0)
@@ -59,7 +66,7 @@ def tile_attend_plw_proto_topk_kernel(tc, qT, k_words, k_scales, c_words, c_scal
 
         nc.sync.dma_start(offsets[:], offs)
         for pool, scales in ((c_scale_pool, c_scales), (k_scale_pool, k_scales)):
-            nc.sync.dma_start(pool[96:P, :].bitcast(I32), scales.rearrange("o f t -> f o t").bitcast(I32))
+            nc.sync.dma_start(pool[LOADED_ROWS:P, :].bitcast(I32), scales.rearrange("o f t -> f o t").bitcast(I32))
         nc.sync.dma_start(c_pool[:].bitcast(I32), c_words[0].rearrange("p t b -> p (t b)").bitcast(I32))
         q_first = load_queries(0, 0, CHUNKS, "first_queries")
         nc.scalar.dma_start(th_rows[0:CHUNKS, :], th[0, 0].rearrange("(j p) -> j p", p=P))
@@ -68,15 +75,16 @@ def tile_attend_plw_proto_topk_kernel(tc, qT, k_words, k_scales, c_words, c_scal
         def gather_scales(pool, plane, name):
             listed = held([P, SLOTS], U8, name)
             nc.vector.tensor_copy(listed[:], pool[:].indirect(offsets[:]))
-            for quad in range(4):
+            rows = SCALE_ROWS * PASSES
+            for quad in range(QUADRANTS):
                 nc.scalar.dma_start(
-                    plane[32 * quad : 32 * quad + 4].bitcast(I32),
-                    listed[96 + 8 * quad : 96 + 8 * quad + 8, :].bitcast(I32),
+                    plane[QUADRANT * quad : QUADRANT * quad + SCALE_ROWS].bitcast(I32),
+                    listed[LOADED_ROWS + rows * quad : LOADED_ROWS + rows * (quad + 1), :].bitcast(I32),
                 )
 
         gather_scales(c_scale_pool, c_scale, "c_scale_listed")
         gather_scales(k_scale_pool, k_scale, "k_scale_listed")
-        q_second = load_queries(1, 0, CHUNKS - 1, "third_pool")
+        q_second = load_queries(1, 0, LAST_CHUNK, "third_pool")
 
         k_pool = []
 
@@ -88,7 +96,7 @@ def tile_attend_plw_proto_topk_kernel(tc, qT, k_words, k_scales, c_words, c_scal
         nc.vector.tensor_copy(c_listed[:], c_pool[:].indirect(offsets[:]))
         load_first_keys(0, "first_pool")
         c_codes = [held([P, 2 * SLOTS], U8, "c_codes%d" % o) for o in range(PASSES)]
-        c_halves = c_listed[:].bitcast(U16).rearrange("p (n h) -> p h n", h=2)
+        c_halves = c_listed[:].bitcast(U16).rearrange("p (n h) -> p h n", h=PASSES)
         for o in range(PASSES):
             nc.vector.tensor_copy(c_codes[o][:].bitcast(U16), c_halves[:, o, :])
         load_first_keys(1, "second_pool")
@@ -104,8 +112,8 @@ def tile_attend_plw_proto_topk_kernel(tc, qT, k_words, k_scales, c_words, c_scal
         def round_queries(o, first, chunks, raw, copy):
             grouped = held([P, chunks * P, PACK], BF16, "q_grouped%d%d" % (o, first))
             copy(
-                grouped[:].rearrange("p (c i) t -> p c t i", i=4),
-                raw.rearrange("p t (c i) -> p c t i", i=4),
+                grouped[:].rearrange("p (c i) t -> p c t i", i=LINE),
+                raw.rearrange("p t (c i) -> p c t i", i=LINE),
             )
             return o, first, chunks, grouped
 
@@ -130,14 +138,14 @@ def tile_attend_plw_proto_topk_kernel(tc, qT, k_words, k_scales, c_words, c_scal
                 stop=(o == PASSES - 1),
             )
 
-        g00 = round_queries(0, 0, 2, q_first[:, :, 0:HALF], nc.scalar.copy)
-        g02 = round_queries(0, 2, 2, q_first[:, :, HALF:QUERIES], nc.scalar.copy)
-        q_last = load_queries(1, CHUNKS - 1, 1, "first_queries")
-        quantize_queries(*g00)
-        g10 = round_queries(1, 0, 2, q_second[:, :, 0:HALF], nc.vector.tensor_copy)
-        quantize_queries(*g02)
-        g12 = round_queries(1, 2, 1, q_second[:, :, HALF : HALF + P], nc.scalar.copy)
-        quantize_queries(*g10)
+        pass0_low = round_queries(0, 0, 2, q_first[:, :, 0:HALF], nc.scalar.copy)
+        pass0_high = round_queries(0, 2, 2, q_first[:, :, HALF:QUERIES], nc.scalar.copy)
+        q_last = load_queries(1, LAST_CHUNK, 1, "first_queries")
+        quantize_queries(*pass0_low)
+        pass1_low = round_queries(1, 0, 2, q_second[:, :, 0:HALF], nc.vector.tensor_copy)
+        quantize_queries(*pass0_high)
+        pass1_third = round_queries(1, 2, 1, q_second[:, :, HALF : HALF + P], nc.scalar.copy)
+        quantize_queries(*pass1_low)
 
         k_codes = [held([P, SLOTS], U32, "k_codes%d" % o) for o in range(PASSES)]
         z_banks = [z_psum.tile([P, SLOTS], F32, name="z_bank", tag="z") for j in range(CHUNKS)]
@@ -161,20 +169,20 @@ def tile_attend_plw_proto_topk_kernel(tc, qT, k_words, k_scales, c_words, c_scal
 
         for j in range(CHUNKS):
             second_scores(j, 0)
-        quantize_queries(*g12)
-        for j in range(CHUNKS - 1):
+        quantize_queries(*pass1_third)
+        for j in range(LAST_CHUNK):
             second_scores(j, 1)
             shift_second_scores(j)
         nc.vector.tensor_copy(k_codes[0][:], k_pool[0][:].indirect(offsets[:]))
         for j in range(CHUNKS):
             first_scores(j, 0)
         nc.vector.tensor_copy(k_codes[1][:], k_pool[1][:].indirect(offsets[:]))
-        quantize_queries(*round_queries(1, CHUNKS - 1, 1, q_last[:], nc.scalar.copy))
-        for j in range(CHUNKS - 1):
+        quantize_queries(*round_queries(1, LAST_CHUNK, 1, q_last[:], nc.scalar.copy))
+        for j in range(LAST_CHUNK):
             first_scores(j, 1)
-        second_scores(CHUNKS - 1, 1)
-        shift_second_scores(CHUNKS - 1)
-        first_scores(CHUNKS - 1, 1)
+        second_scores(LAST_CHUNK, 1)
+        shift_second_scores(LAST_CHUNK)
+        first_scores(LAST_CHUNK, 1)
 
         y_codes = held([P, QUERIES], U32, "y_codes")
         y_scale = held([P, QUERIES], U8, "y_scale")
@@ -202,10 +210,12 @@ def tile_attend_plw_proto_topk_kernel(tc, qT, k_words, k_scales, c_words, c_scal
         def hand_on(j):
             cols = slice(j * P, (j + 1) * P)
             grouped = held([P, P, PACK], BF16, "y_grouped%d" % j)
-            nc.vector.tensor_copy(
-                grouped[:].rearrange("p (c i) r -> p c r i", i=4),
-                weights[j][:].rearrange("p r (c i) -> p c r i", i=4),
-            )
+            rounded = grouped[:].rearrange("p (c i) r -> p c r i", i=LINE)
+            stored = weights[j][:].rearrange("p r (c i) -> p c r i", i=LINE)
+            if j == 0:
+                nc.gpsimd.tensor_scalar(out=rounded, in0=stored, scalar1=1.0, scalar2=0.0, op0=ALU.mult, op1=ALU.add)
+            else:
+                nc.vector.tensor_copy(rounded, stored)
             nc.vector.quantize_mx(
                 out=y_codes[:, cols].bitcast(FP8X4), scales=y_scale[:, cols], in_=grouped[:].rearrange("p q r -> p (q r)")
             )
@@ -217,8 +227,9 @@ def tile_attend_plw_proto_topk_kernel(tc, qT, k_words, k_scales, c_words, c_scal
             weigh(j)
         for j in range(CHUNKS):
             hand_on(j)
-        for quad in range(4):
+        for quad in range(QUADRANTS):
             queue = nc.scalar if quad % 2 == 0 else nc.sync
             queue.dma_start(
-                out_2[0, 4 * quad : 4 * quad + 4, :].bitcast(I32), y_scale[32 * quad : 32 * quad + 4, :].bitcast(I32)
+                out_2[0, SCALE_ROWS * quad : SCALE_ROWS * (quad + 1), :].bitcast(I32),
+                y_scale[QUADRANT * quad : QUADRANT * quad + SCALE_ROWS, :].bitcast(I32),
             )

@@ -34,8 +34,8 @@ def tile_attend_plw_proto_topk_kernel(tc, qT, k_words, k_scales, c_words, c_scal
     nc = tc.nc
     with ExitStack() as ctx:
         keep = ctx.enter_context(tc.tile_pool(name="keep", bufs=1))
-        a_psum = ctx.enter_context(tc.psum_pool(name="a_psum", bufs=CHUNKS))
-        z_psum = ctx.enter_context(tc.psum_pool(name="z_psum", bufs=CHUNKS))
+        a_psum = ctx.enter_context(tc.psum_pool(name="a_psum", bufs=CHUNKS + 1))
+        z_psum = ctx.enter_context(tc.psum_pool(name="z_psum", bufs=CHUNKS - 1))
 
         def held(shape, dtype, name, tag=None):
             return keep.tile(shape, dtype, name=name, tag=tag or name, align_bytes=64)
@@ -84,7 +84,7 @@ def tile_attend_plw_proto_topk_kernel(tc, qT, k_words, k_scales, c_words, c_scal
 
         gather_scales(c_scale_pool, c_scale, "c_scale_listed")
         gather_scales(k_scale_pool, k_scale, "k_scale_listed")
-        q_second = load_queries(1, 0, LAST_CHUNK, "third_pool")
+        q_second = load_queries(1, 0, CHUNKS, "third_pool")
 
         k_pool = []
 
@@ -140,23 +140,27 @@ def tile_attend_plw_proto_topk_kernel(tc, qT, k_words, k_scales, c_words, c_scal
 
         pass0_low = round_queries(0, 0, 2, q_first[:, :, 0:HALF], nc.scalar.copy)
         pass0_high = round_queries(0, 2, 2, q_first[:, :, HALF:QUERIES], nc.scalar.copy)
-        q_last = load_queries(1, LAST_CHUNK, 1, "first_queries")
         quantize_queries(*pass0_low)
         pass1_low = round_queries(1, 0, 2, q_second[:, :, 0:HALF], nc.vector.tensor_copy)
         quantize_queries(*pass0_high)
-        pass1_third = round_queries(1, 2, 1, q_second[:, :, HALF : HALF + P], nc.scalar.copy)
+        pass1_high = round_queries(1, 2, 2, q_second[:, :, HALF:QUERIES], nc.scalar.copy)
         quantize_queries(*pass1_low)
 
         k_codes = [held([P, SLOTS], U32, "k_codes%d" % o) for o in range(PASSES)]
-        z_banks = [z_psum.tile([P, SLOTS], F32, name="z_bank", tag="z") for j in range(CHUNKS)]
-        a_banks = [a_psum.tile([P, SLOTS], F32, name="a_bank", tag="a") for j in range(CHUNKS)]
+        z_banks = {}
+        a_parts = [[(h * HALF, HALF, a_psum.tile([P, HALF], F32, name="a_half", tag="a")) for h in range(2)]]
+        a_parts.extend([(0, SLOTS, a_psum.tile([P, SLOTS], F32, name="a_bank", tag="a"))] for j in range(1, CHUNKS))
         z_less_th = {}
 
         def second_scores(j, o):
+            if o == 0:
+                z_banks[j] = z_psum.tile([P, SLOTS], F32, name="z_bank", tag="z")
             scores(z_banks[j], j, o, c_codes[o][:].bitcast(FP4X4), c_scale[:, o, :])
 
         def first_scores(j, o):
-            scores(a_banks[j], j, o, k_codes[o][:].bitcast(FP8X4), k_scale[:, o, :])
+            for first, count, bank in a_parts[j]:
+                cols = slice(first, first + count)
+                scores(bank, j, o, k_codes[o][:, cols].bitcast(FP8X4), k_scale[:, o, cols])
 
         def shift_second_scores(j):
             z_less_th[j] = held([P, PACK, P], F32, "z_less_th%d" % j)
@@ -167,69 +171,84 @@ def tile_attend_plw_proto_topk_kernel(tc, qT, k_words, k_scales, c_words, c_scal
                 bias=minus_th[:, j : j + 1],
             )
 
-        for j in range(CHUNKS):
-            second_scores(j, 0)
-        quantize_queries(*pass1_third)
         for j in range(LAST_CHUNK):
+            second_scores(j, 0)
+        quantize_queries(*pass1_high)
+        for j in range(CHUNKS):
+            if j == LAST_CHUNK:
+                second_scores(j, 0)
             second_scores(j, 1)
             shift_second_scores(j)
         nc.vector.tensor_copy(k_codes[0][:], k_pool[0][:].indirect(offsets[:]))
         for j in range(CHUNKS):
             first_scores(j, 0)
-        nc.vector.tensor_copy(k_codes[1][:], k_pool[1][:].indirect(offsets[:]))
-        quantize_queries(*round_queries(1, LAST_CHUNK, 1, q_last[:], nc.scalar.copy))
-        for j in range(LAST_CHUNK):
+        for h in range(2):
+            listed = offsets[:, h * HALF // 16 : (h + 1) * HALF // 16]
+            nc.vector.tensor_copy(k_codes[1][:, h * HALF : (h + 1) * HALF], k_pool[1][:].indirect(listed))
+        for j in range(CHUNKS):
             first_scores(j, 1)
-        second_scores(LAST_CHUNK, 1)
-        shift_second_scores(LAST_CHUNK)
-        first_scores(LAST_CHUNK, 1)
 
         y_codes = held([P, QUERIES], U32, "y_codes")
         y_scale = held([P, QUERIES], U8, "y_scale")
         y_rows = out_0.rearrange("(p r) q -> p r q", r=PACK)
         word_rows = out_1[0].rearrange("p q b -> p (q b)").bitcast(I32)
-        weights = {}
+        last_pair = held([P, PACK, HALF], F32, "last_pair")
+        weights = [held([P, PACK, P], F32, "weights%d" % j)[:] for j in range(2)]
+        weights.extend([last_pair[:, :, 0:P], last_pair[:, :, P:HALF]])
+        bests = {}
+
+        calls = ((0, 2), (2, 1), (3, 1))
+        grouped = {first: held([P, count * P, PACK], BF16, "y_grouped%d" % first) for first, count in calls}
+
+        def rounded(j):
+            return grouped[0][:, j * P : (j + 1) * P, :] if j < 2 else grouped[j][:]
 
         def weigh(j):
             best = held([P, PACK, P], F32, "best%d" % j)
-            nc.vector.scalar_tensor_tensor(
-                out=best[:],
-                in0=a_banks[j][:].rearrange("p (s r) -> p r s", r=PACK),
-                scalar=minus_th[:, j : j + 1],
-                in1=z_less_th[j][:],
-                op0=ALU.add,
-                op1=ALU.max,
-            )
+            bests[j] = best
+            for first, count, bank in a_parts[j]:
+                rows = slice(first // PACK, (first + count) // PACK)
+                nc.vector.scalar_tensor_tensor(
+                    out=best[:, :, rows],
+                    in0=bank[:].rearrange("p (s r) -> p r s", r=PACK),
+                    scalar=minus_th[:, j : j + 1],
+                    in1=z_less_th[j][:, :, rows],
+                    op0=ALU.add,
+                    op1=ALU.max,
+                )
             turned = z_psum.tile([P, PACK, P], F32, name="turned", tag="z")
             for r in range(PACK):
                 nc.tensor.transpose(turned[:, r, :], best[:, r, :], identity[:])
-            weights[j] = held([P, PACK, P], F32, "weights%d" % j)
-            nc.scalar.activation(out=weights[j][:], in_=turned[:], func=ACT.Sigmoid)
-            nc.sync.dma_start(y_rows[:, :, j * P : (j + 1) * P], weights[j][:])
+            nc.scalar.activation(out=weights[j], in_=turned[:], func=ACT.Sigmoid)
+            if j < 2:
+                nc.sync.dma_start(y_rows[:, :, j * P : (j + 1) * P], weights[j])
+            elif j == LAST_CHUNK:
+                nc.sync.dma_start(y_rows[:, :, HALF:QUERIES], last_pair[:])
 
-        def hand_on(j):
-            cols = slice(j * P, (j + 1) * P)
-            grouped = held([P, P, PACK], BF16, "y_grouped%d" % j)
-            rounded = grouped[:].rearrange("p (c i) r -> p c r i", i=LINE)
-            stored = weights[j][:].rearrange("p r (c i) -> p c r i", i=LINE)
-            if j == 0:
-                nc.gpsimd.tensor_scalar(out=rounded, in0=stored, scalar1=1.0, scalar2=0.0, op0=ALU.mult, op1=ALU.add)
-            else:
-                nc.vector.tensor_copy(rounded, stored)
-            nc.vector.quantize_mx(
-                out=y_codes[:, cols].bitcast(FP8X4), scales=y_scale[:, cols], in_=grouped[:].rearrange("p q r -> p (q r)")
+        def round_weights(j):
+            nc.vector.tensor_copy(
+                rounded(j).rearrange("p (c i) r -> p c r i", i=LINE),
+                weights[j].rearrange("p r (c i) -> p c r i", i=LINE),
             )
-            if j % 2 == 1:
-                pair = slice((j - 1) * P, (j + 1) * P)
-                nc.sync.dma_start(word_rows[:, pair], y_codes[:, pair].bitcast(I32))
+
+        def hand_on(first, count):
+            cols = slice(first * P, (first + count) * P)
+            nc.vector.quantize_mx(
+                out=y_codes[:, cols].bitcast(FP8X4), scales=y_scale[:, cols], in_=grouped[first][:].rearrange("p q r -> p (q r)")
+            )
 
         for j in range(CHUNKS):
             weigh(j)
-        for j in range(CHUNKS):
-            hand_on(j)
+        round_weights(0)
+        round_weights(1)
+        round_weights(2)
+        hand_on(*calls[0])
+        round_weights(LAST_CHUNK)
+        hand_on(*calls[1])
+        hand_on(*calls[2])
+        nc.sync.dma_start(word_rows, y_codes[:].bitcast(I32))
         for quad in range(QUADRANTS):
-            queue = nc.scalar if quad % 2 == 0 else nc.sync
-            queue.dma_start(
+            nc.scalar.dma_start(
                 out_2[0, SCALE_ROWS * quad : SCALE_ROWS * (quad + 1), :].bitcast(I32),
                 y_scale[QUADRANT * quad : QUADRANT * quad + SCALE_ROWS, :].bitcast(I32),
             )

@@ -34,15 +34,17 @@ def tile_attend_plw_proto_topk_kernel(tc, qT, k_words, k_scales, c_words, c_scal
     nc = tc.nc
     with ExitStack() as ctx:
         keep = ctx.enter_context(tc.tile_pool(name="keep", bufs=1))
-        a_psum = ctx.enter_context(tc.psum_pool(name="a_psum", bufs=CHUNKS + 1))
-        z_psum = ctx.enter_context(tc.psum_pool(name="z_psum", bufs=CHUNKS - 1))
+        psum = ctx.enter_context(tc.psum_pool(name="psum", bufs=1))
+
+        def bank(shape, name, number):
+            return psum.tile(shape, F32, name=name, tag="bank%d" % number)
 
         def held(shape, dtype, name, tag=None):
             return keep.tile(shape, dtype, name=name, tag=tag or name, align_bytes=64)
 
         offsets = held([P, SLOTS // 16], U16, "offsets")
         c_pool = held([P, TOKENS], U32, "c_pool", "first_pool")
-        c_scale_pool = held([P, TOKENS], U8, "c_scale_pool")
+        c_scale_pool = held([P, TOKENS], U8, "c_scale_pool", "second_queries")
         k_scale_pool = held([P, TOKENS], U8, "k_scale_pool", "third_pool")
         c_scale = held([P, PASSES, SLOTS], U8, "c_scale")
         k_scale = held([P, PASSES, SLOTS], U8, "k_scale")
@@ -72,19 +74,22 @@ def tile_attend_plw_proto_topk_kernel(tc, qT, k_words, k_scales, c_words, c_scal
         nc.scalar.dma_start(th_rows[0:CHUNKS, :], th[0, 0].rearrange("(j p) -> j p", p=P))
         nc.scalar.activation(out=warm[:, 8:9], in_=warm[:, 0:1], func=ACT.Sigmoid)
 
-        def gather_scales(pool, plane, name):
+        def gather_scales(pool, name):
             listed = held([P, SLOTS], U8, name)
             nc.vector.tensor_copy(listed[:], pool[:].indirect(offsets[:]))
+            return listed
+
+        def move_scales(listed, plane):
             rows = SCALE_ROWS * PASSES
             for quad in range(QUADRANTS):
-                nc.scalar.dma_start(
+                nc.sync.dma_start(
                     plane[QUADRANT * quad : QUADRANT * quad + SCALE_ROWS].bitcast(I32),
                     listed[LOADED_ROWS + rows * quad : LOADED_ROWS + rows * (quad + 1), :].bitcast(I32),
                 )
 
-        gather_scales(c_scale_pool, c_scale, "c_scale_listed")
-        gather_scales(k_scale_pool, k_scale, "k_scale_listed")
-        q_second = load_queries(1, 0, CHUNKS, "third_pool")
+        move_scales(gather_scales(c_scale_pool, "c_scale_listed"), c_scale)
+        q_second = load_queries(1, 0, CHUNKS, "second_queries")
+        k_scale_listed = gather_scales(k_scale_pool, "k_scale_listed")
 
         k_pool = []
 
@@ -92,16 +97,18 @@ def tile_attend_plw_proto_topk_kernel(tc, qT, k_words, k_scales, c_words, c_scal
             k_pool.append(held([P, TOKENS], U32, "k_pool%d" % o, tag))
             nc.sync.dma_start(k_pool[o][:].bitcast(I32), k_words[o].rearrange("p t b -> p (t b)").bitcast(I32))
 
-        c_listed = held([P, SLOTS], U32, "c_listed", "second_pool")
+        load_first_keys(0, "third_pool")
+        move_scales(k_scale_listed, k_scale)
+
+        c_listed = held([P, SLOTS], U32, "c_listed")
         nc.vector.tensor_copy(c_listed[:], c_pool[:].indirect(offsets[:]))
-        load_first_keys(0, "first_pool")
         c_codes = [held([P, 2 * SLOTS], U8, "c_codes%d" % o) for o in range(PASSES)]
         c_halves = c_listed[:].bitcast(U16).rearrange("p (n h) -> p h n", h=PASSES)
         for o in range(PASSES):
             nc.vector.tensor_copy(c_codes[o][:].bitcast(U16), c_halves[:, o, :])
-        load_first_keys(1, "second_pool")
+        load_first_keys(1, "first_pool")
 
-        th_turned = z_psum.tile([P, P], F32, name="th_turned", tag="z")
+        th_turned = bank([P, P], "th_turned", 1)
         nc.tensor.transpose(th_turned[:], th_rows[:], identity[:])
         minus_th = held([P, CHUNKS], F32, "minus_th")
         nc.vector.tensor_scalar(out=minus_th[:], in0=th_turned[:, 0:CHUNKS], scalar1=-1.0, scalar2=None, op0=ALU.mult)
@@ -127,9 +134,9 @@ def tile_attend_plw_proto_topk_kernel(tc, qT, k_words, k_scales, c_words, c_scal
                 q_codes[o, first + c] = codes[:, c * P : (c + 1) * P]
                 q_scale[o, first + c] = scale[:, c * P : (c + 1) * P]
 
-        def scores(bank, j, o, codes, scale):
+        def scores(sums, j, o, codes, scale):
             nc.tensor.matmul_mx(
-                out=bank[:],
+                out=sums[:],
                 lhsT=q_codes[o, j].bitcast(FP8X4),
                 lhsT_scale=q_scale[o, j],
                 rhs=codes,
@@ -138,55 +145,74 @@ def tile_attend_plw_proto_topk_kernel(tc, qT, k_words, k_scales, c_words, c_scal
                 stop=(o == PASSES - 1),
             )
 
-        pass0_low = round_queries(0, 0, 2, q_first[:, :, 0:HALF], nc.scalar.copy)
-        pass0_high = round_queries(0, 2, 2, q_first[:, :, HALF:QUERIES], nc.scalar.copy)
+        pass0_low = round_queries(0, 2, 2, q_first[:, :, HALF:QUERIES], nc.scalar.copy)
+        pass0_high = round_queries(0, 0, 2, q_first[:, :, 0:HALF], nc.scalar.copy)
         quantize_queries(*pass0_low)
-        pass1_low = round_queries(1, 0, 2, q_second[:, :, 0:HALF], nc.vector.tensor_copy)
+        pass1_low = round_queries(1, 2, 2, q_second[:, :, HALF:QUERIES], nc.vector.tensor_copy)
         quantize_queries(*pass0_high)
-        pass1_high = round_queries(1, 2, 2, q_second[:, :, HALF:QUERIES], nc.scalar.copy)
+        pass1_high = round_queries(1, 0, 2, q_second[:, :, 0:HALF], nc.scalar.copy)
         quantize_queries(*pass1_low)
 
         k_codes = [held([P, SLOTS], U32, "k_codes%d" % o) for o in range(PASSES)]
         z_banks = {}
-        a_parts = [[(h * HALF, HALF, a_psum.tile([P, HALF], F32, name="a_half", tag="a")) for h in range(2)]]
-        a_parts.extend([(0, SLOTS, a_psum.tile([P, SLOTS], F32, name="a_bank", tag="a"))] for j in range(1, CHUNKS))
         z_less_th = {}
 
         def second_scores(j, o):
             if o == 0:
-                z_banks[j] = z_psum.tile([P, SLOTS], F32, name="z_bank", tag="z")
+                z_banks[j] = bank([P, SLOTS], "z_bank", (7, 5, 6, 5)[j])
             scores(z_banks[j], j, o, c_codes[o][:].bitcast(FP4X4), c_scale[:, o, :])
 
         def first_scores(j, o):
-            for first, count, bank in a_parts[j]:
+            for first, count, part in a_parts[j]:
                 cols = slice(first, first + count)
-                scores(bank, j, o, k_codes[o][:, cols].bitcast(FP8X4), k_scale[:, o, cols])
+                scores(part, j, o, k_codes[o][:, cols].bitcast(FP8X4), k_scale[:, o, cols])
 
         def shift_second_scores(j):
             z_less_th[j] = held([P, PACK, P], F32, "z_less_th%d" % j)
             nc.scalar.activation(
                 out=z_less_th[j][:],
                 in_=z_banks[j][:].rearrange("p (s r) -> p r s", r=PACK),
-                func=ACT.Identity,
+                func=ACT.Sigmoid if j == LAST_CHUNK else ACT.Identity,
                 bias=minus_th[:, j : j + 1],
             )
 
-        for j in range(LAST_CHUNK):
+        def turn(dealt, number):
+            turned = bank([P, PACK, P], "turned", number)
+            for r in range(PACK):
+                nc.tensor.transpose(turned[:, r, :], dealt[:, r, :], identity[:])
+            return turned
+
+        for j in (3, 2, 0):
             second_scores(j, 0)
         quantize_queries(*pass1_high)
-        for j in range(CHUNKS):
-            if j == LAST_CHUNK:
-                second_scores(j, 0)
+        for j in (3, 2):
             second_scores(j, 1)
             shift_second_scores(j)
+        z_weights = held([P, PACK, P], F32, "z_weights")
+        z_turned = turn(z_less_th[LAST_CHUNK], 0)
+        second_scores(0, 1)
+        shift_second_scores(0)
+        nc.scalar.copy(z_weights[:], z_turned[:])
+        second_scores(1, 0)
+        second_scores(1, 1)
+        shift_second_scores(1)
+        a_parts = [[(h * HALF, HALF, bank([P, HALF], "a_half", h)) for h in range(2)]]
+        a_parts.extend([(0, SLOTS, bank([P, SLOTS], "a_bank", j + 1))] for j in range(1, CHUNKS))
         nc.vector.tensor_copy(k_codes[0][:], k_pool[0][:].indirect(offsets[:]))
         for j in range(CHUNKS):
             first_scores(j, 0)
         for h in range(2):
             listed = offsets[:, h * HALF // 16 : (h + 1) * HALF // 16]
             nc.vector.tensor_copy(k_codes[1][:, h * HALF : (h + 1) * HALF], k_pool[1][:].indirect(listed))
-        for j in range(CHUNKS):
+        for j in (0, LAST_CHUNK, 1, 2):
             first_scores(j, 1)
+        a_weights = held([P, PACK, P], F32, "a_weights")
+        nc.scalar.activation(
+            out=a_weights[:],
+            in_=a_parts[LAST_CHUNK][0][2][:].rearrange("p (s r) -> p r s", r=PACK),
+            func=ACT.Sigmoid,
+            bias=minus_th[:, LAST_CHUNK : LAST_CHUNK + 1],
+        )
 
         y_codes = held([P, QUERIES], U32, "y_codes")
         y_scale = held([P, QUERIES], U8, "y_scale")
@@ -206,24 +232,23 @@ def tile_attend_plw_proto_topk_kernel(tc, qT, k_words, k_scales, c_words, c_scal
         def weigh(j):
             best = held([P, PACK, P], F32, "best%d" % j)
             bests[j] = best
-            for first, count, bank in a_parts[j]:
+            for first, count, part in a_parts[j]:
                 rows = slice(first // PACK, (first + count) // PACK)
                 nc.vector.scalar_tensor_tensor(
                     out=best[:, :, rows],
-                    in0=bank[:].rearrange("p (s r) -> p r s", r=PACK),
+                    in0=part[:].rearrange("p (s r) -> p r s", r=PACK),
                     scalar=minus_th[:, j : j + 1],
                     in1=z_less_th[j][:, :, rows],
                     op0=ALU.add,
                     op1=ALU.max,
                 )
-            turned = z_psum.tile([P, PACK, P], F32, name="turned", tag="z")
-            for r in range(PACK):
-                nc.tensor.transpose(turned[:, r, :], best[:, r, :], identity[:])
+            turned = turn(best, 5 + j)
             nc.scalar.activation(out=weights[j], in_=turned[:], func=ACT.Sigmoid)
+            if j == 2:
+                nc.scalar.activation(out=rounded(j), in_=turned[:].rearrange("p r q -> p q r"), func=ACT.Sigmoid)
             if j < 2:
                 nc.sync.dma_start(y_rows[:, :, j * P : (j + 1) * P], weights[j])
-            elif j == LAST_CHUNK:
-                nc.sync.dma_start(y_rows[:, :, HALF:QUERIES], last_pair[:])
+
 
         def round_weights(j):
             nc.vector.tensor_copy(
@@ -237,15 +262,18 @@ def tile_attend_plw_proto_topk_kernel(tc, qT, k_words, k_scales, c_words, c_scal
                 out=y_codes[:, cols].bitcast(FP8X4), scales=y_scale[:, cols], in_=grouped[first][:].rearrange("p q r -> p (q r)")
             )
 
-        for j in range(CHUNKS):
-            weigh(j)
+        weigh(0)
+        weigh(1)
+        a_turned = turn(a_weights, 2)
+        weigh(2)
         round_weights(0)
+        nc.vector.tensor_tensor(out=weights[LAST_CHUNK], in0=a_turned[:], in1=z_weights[:], op=ALU.max)
+        nc.sync.dma_start(y_rows[:, :, HALF:QUERIES], last_pair[:])
         round_weights(1)
-        round_weights(2)
-        hand_on(*calls[0])
         round_weights(LAST_CHUNK)
-        hand_on(*calls[1])
+        hand_on(*calls[0])
         hand_on(*calls[2])
+        hand_on(*calls[1])
         nc.sync.dma_start(word_rows, y_codes[:].bitcast(I32))
         for quad in range(QUADRANTS):
             nc.scalar.dma_start(

@@ -204,7 +204,7 @@ def tile_attend_plw_proto_topk_kernel(tc, qT, k_words, k_scales, c_words, c_scal
         for h in range(2):
             listed = offsets[:, h * HALF // 16 : (h + 1) * HALF // 16]
             nc.vector.tensor_copy(k_codes[1][:, h * HALF : (h + 1) * HALF], k_pool[1][:].indirect(listed))
-        for j in (0, LAST_CHUNK, 1, 2):
+        for j in (0, 1, LAST_CHUNK, 2):
             first_scores(j, 1)
         a_weights = held([P, PACK, P], F32, "a_weights")
         nc.scalar.activation(
@@ -219,9 +219,9 @@ def tile_attend_plw_proto_topk_kernel(tc, qT, k_words, k_scales, c_words, c_scal
         y_rows = out_0.rearrange("(p r) q -> p r q", r=PACK)
         word_rows = out_1[0].rearrange("p q b -> p (q b)").bitcast(I32)
         last_pair = held([P, PACK, HALF], F32, "last_pair")
-        weights = [held([P, PACK, P], F32, "weights%d" % j)[:] for j in range(2)]
+        first_pair = held([P, PACK, HALF], F32, "first_pair")
+        weights = [first_pair[:, :, 0:P], first_pair[:, :, P:HALF]]
         weights.extend([last_pair[:, :, 0:P], last_pair[:, :, P:HALF]])
-        bests = {}
 
         calls = ((0, 2), (2, 1), (3, 1))
         grouped = {first: held([P, count * P, PACK], BF16, "y_grouped%d" % first) for first, count in calls}
@@ -229,26 +229,36 @@ def tile_attend_plw_proto_topk_kernel(tc, qT, k_words, k_scales, c_words, c_scal
         def rounded(j):
             return grouped[0][:, j * P : (j + 1) * P, :] if j < 2 else grouped[j][:]
 
-        def weigh(j):
-            best = held([P, PACK, P], F32, "best%d" % j)
-            bests[j] = best
-            for first, count, part in a_parts[j]:
-                rows = slice(first // PACK, (first + count) // PACK)
-                nc.vector.scalar_tensor_tensor(
-                    out=best[:, :, rows],
-                    in0=part[:].rearrange("p (s r) -> p r s", r=PACK),
-                    scalar=minus_th[:, j : j + 1],
-                    in1=z_less_th[j][:, :, rows],
-                    op0=ALU.add,
-                    op1=ALU.max,
-                )
-            turned = turn(best, 5 + j)
-            nc.scalar.activation(out=weights[j], in_=turned[:], func=ACT.Sigmoid)
-            if j == 2:
-                nc.scalar.activation(out=rounded(j), in_=turned[:].rearrange("p r q -> p q r"), func=ACT.Sigmoid)
-            if j < 2:
-                nc.sync.dma_start(y_rows[:, :, j * P : (j + 1) * P], weights[j])
+        best = [held([P, PACK, P], F32, "best%d" % j) for j in range(LAST_CHUNK)]
 
+        def take_best(j, number, places):
+            first, count, part = a_parts[j][number]
+            rows = slice(first // PACK, (first + count) // PACK)
+            nc.vector.scalar_tensor_tensor(
+                out=best[j][:, places, rows],
+                in0=part[:].rearrange("p (s r) -> p r s", r=PACK)[:, places, :],
+                scalar=minus_th[:, j : j + 1],
+                in1=z_less_th[j][:, places, rows],
+                op0=ALU.add,
+                op1=ALU.max,
+            )
+
+        def weigh_first_pair(g):
+            places = slice(2 * g, 2 * g + 2)
+            take_best(0, 1, places)
+            take_best(1, 0, places)
+            turned = bank([P, 2, HALF], "turned_pair", 5 + g)
+            for r in range(2):
+                for j in range(2):
+                    nc.tensor.transpose(turned[:, r, j * P : (j + 1) * P], best[j][:, 2 * g + r, :], identity[:])
+            nc.scalar.activation(out=first_pair[:, places, :], in_=turned[:], func=ACT.Sigmoid)
+            nc.sync.dma_start(y_rows[:, places, 0:HALF], first_pair[:, places, :])
+
+        def weigh(j):
+            take_best(j, 0, slice(0, PACK))
+            turned = turn(best[j], 5 + j)
+            nc.scalar.activation(out=weights[j], in_=turned[:], func=ACT.Sigmoid)
+            nc.scalar.activation(out=rounded(j), in_=turned[:].rearrange("p r q -> p q r"), func=ACT.Sigmoid)
 
         def round_weights(j):
             nc.vector.tensor_copy(
@@ -262,14 +272,17 @@ def tile_attend_plw_proto_topk_kernel(tc, qT, k_words, k_scales, c_words, c_scal
                 out=y_codes[:, cols].bitcast(FP8X4), scales=y_scale[:, cols], in_=grouped[first][:].rearrange("p q r -> p (q r)")
             )
 
-        weigh(0)
-        weigh(1)
+        take_best(0, 0, slice(0, PACK))
+        weigh_first_pair(0)
+        weigh_first_pair(1)
         a_turned = turn(a_weights, 2)
         weigh(2)
-        round_weights(0)
         nc.vector.tensor_tensor(out=weights[LAST_CHUNK], in0=a_turned[:], in1=z_weights[:], op=ALU.max)
         nc.sync.dma_start(y_rows[:, :, HALF:QUERIES], last_pair[:])
-        round_weights(1)
+        nc.vector.tensor_copy(
+            grouped[0][:].rearrange("p (c i) r -> p c r i", i=LINE),
+            first_pair[:].rearrange("p r (c i) -> p c r i", i=LINE),
+        )
         round_weights(LAST_CHUNK)
         hand_on(*calls[0])
         hand_on(*calls[2])

@@ -26,7 +26,8 @@ PASSES = FEATURES // PASS_FEATURES
 CHUNKS = QUERIES // P
 LAST_CHUNK = CHUNKS - 1
 HALF = QUERIES // 2
-LOADED_ROWS = P - QUADRANT
+C_LOADED, K_LOADED = QUADRANT, P - QUADRANT
+K_PLANE = SCALE_ROWS
 FLOPS = 2 * 2 * SLOTS * FEATURES * QUERIES
 
 
@@ -59,16 +60,19 @@ def tile_attend_plw_proto_topk_kernel(tc, qT, k_words, k_scales, c_words, c_scal
             return raw
 
         nc.vector.memset(warm[:, 0:1], 0.0)
-        for pool in (c_scale_pool, k_scale_pool):
-            nc.vector.memset(pool[0:LOADED_ROWS, :].bitcast(I32), 0)
+        nc.vector.memset(c_scale_pool[0:C_LOADED, :].bitcast(I32), 0)
+        nc.vector.memset(c_scale_pool[C_LOADED + QUADRANT : P, :].bitcast(I32), 0)
+        nc.vector.memset(k_scale_pool[0:K_LOADED, :].bitcast(I32), 0)
         for plane in (c_scale, k_scale):
             nc.vector.memset(plane[:].rearrange("p o n -> p (o n)").bitcast(I32), 0)
         nc.gpsimd.memset(th_rows[:], 0.0)
         make_identity(nc, identity[:])
 
         nc.sync.dma_start(offsets[:], offs)
-        for pool, scales in ((c_scale_pool, c_scales), (k_scale_pool, k_scales)):
-            nc.sync.dma_start(pool[LOADED_ROWS:P, :].bitcast(I32), scales.rearrange("o f t -> f o t").bitcast(I32))
+        for pool, scales, loaded in ((c_scale_pool, c_scales, C_LOADED), (k_scale_pool, k_scales, K_LOADED)):
+            nc.sync.dma_start(
+                pool[loaded : loaded + QUADRANT, :].bitcast(I32), scales.rearrange("o f t -> f o t").bitcast(I32)
+            )
         nc.sync.dma_start(c_pool[:].bitcast(I32), c_words[0].rearrange("p t b -> p (t b)").bitcast(I32))
         q_first = load_queries(0, 0, CHUNKS, "first_queries")
         nc.scalar.dma_start(th_rows[0:CHUNKS, :], th[0, 0].rearrange("(j p) -> j p", p=P))
@@ -79,15 +83,15 @@ def tile_attend_plw_proto_topk_kernel(tc, qT, k_words, k_scales, c_words, c_scal
             nc.vector.tensor_copy(listed[:], pool[:].indirect(offsets[:]))
             return listed
 
-        def move_scales(listed, plane):
+        def move_scales(listed, loaded, plane, start):
             rows = SCALE_ROWS * PASSES
             for quad in range(QUADRANTS):
                 nc.sync.dma_start(
-                    plane[QUADRANT * quad : QUADRANT * quad + SCALE_ROWS].bitcast(I32),
-                    listed[LOADED_ROWS + rows * quad : LOADED_ROWS + rows * (quad + 1), :].bitcast(I32),
+                    plane[QUADRANT * quad + start : QUADRANT * quad + start + SCALE_ROWS].bitcast(I32),
+                    listed[loaded + rows * quad : loaded + rows * (quad + 1), :].bitcast(I32),
                 )
 
-        move_scales(gather_scales(c_scale_pool, "c_scale_listed"), c_scale)
+        move_scales(gather_scales(c_scale_pool, "c_scale_listed"), C_LOADED, c_scale, 0)
         q_second = load_queries(1, 0, CHUNKS, "second_queries")
         k_scale_listed = gather_scales(k_scale_pool, "k_scale_listed")
 
@@ -98,7 +102,7 @@ def tile_attend_plw_proto_topk_kernel(tc, qT, k_words, k_scales, c_words, c_scal
             nc.sync.dma_start(k_pool[o][:].bitcast(I32), k_words[o].rearrange("p t b -> p (t b)").bitcast(I32))
 
         load_first_keys(0, "third_pool")
-        move_scales(k_scale_listed, k_scale)
+        move_scales(k_scale_listed, K_LOADED, k_scale, K_PLANE)
 
         c_listed = held([P, SLOTS], U32, "c_listed")
         nc.vector.tensor_copy(c_listed[:], c_pool[:].indirect(offsets[:]))
@@ -165,7 +169,7 @@ def tile_attend_plw_proto_topk_kernel(tc, qT, k_words, k_scales, c_words, c_scal
         def first_scores(j, o):
             for first, count, part in a_parts[j]:
                 cols = slice(first, first + count)
-                scores(part, j, o, k_codes[o][:, cols].bitcast(FP8X4), k_scale[:, o, cols])
+                scores(part, j, o, k_codes[o][:, cols].bitcast(FP8X4), k_scale[K_PLANE:P, o, cols])
 
         def shift_second_scores(j):
             z_less_th[j] = held([P, PACK, P], F32, "z_less_th%d" % j)

@@ -163,11 +163,11 @@ def tile_attend_plw_proto_topk_kernel(tc, qT, k_words, k_scales, c_words, c_scal
 
         def second_scores(j, o):
             if o == 0:
-                z_banks[j] = bank([P, SLOTS], "z_bank", (7, 5, 6, 5)[j])
+                z_banks[j] = bank([P, SLOTS], "z_bank", (7, 7, 4, 5)[j])
             scores(z_banks[j], j, o, c_codes[o][:].bitcast(FP4X4), c_scale[:, o, :])
 
-        def first_scores(j, o):
-            for first, count, part in a_parts[j]:
+        def first_scores(j, o, parts=slice(None)):
+            for first, count, part in a_parts[j][parts]:
                 cols = slice(first, first + count)
                 scores(part, j, o, k_codes[o][:, cols].bitcast(FP8X4), k_scale[K_PLANE:P, o, cols])
 
@@ -193,22 +193,24 @@ def tile_attend_plw_proto_topk_kernel(tc, qT, k_words, k_scales, c_words, c_scal
             second_scores(j, 1)
             shift_second_scores(j)
         z_weights = held([P, PACK, P], F32, "z_weights")
-        z_turned = turn(z_less_th[LAST_CHUNK], 0)
+        z_turned = turn(z_less_th[LAST_CHUNK], 6)
         second_scores(0, 1)
         shift_second_scores(0)
         nc.scalar.copy(z_weights[:], z_turned[:])
         second_scores(1, 0)
         second_scores(1, 1)
         shift_second_scores(1)
-        a_parts = [[(h * HALF, HALF, bank([P, HALF], "a_half", h)) for h in range(2)]]
-        a_parts.extend([(0, SLOTS, bank([P, SLOTS], "a_bank", j + 1))] for j in range(1, CHUNKS))
+        a_parts = [[(h * HALF, HALF, bank([P, HALF], "a_half", 2 * j + h)) for h in range(2)] for j in range(2)]
+        a_parts.extend([(0, SLOTS, bank([P, SLOTS], "a_bank", j + 2))] for j in range(2, CHUNKS))
         nc.vector.tensor_copy(k_codes[0][:], k_pool[0][:].indirect(offsets[:]))
         for j in range(CHUNKS):
             first_scores(j, 0)
         for h in range(2):
             listed = offsets[:, h * HALF // 16 : (h + 1) * HALF // 16]
             nc.vector.tensor_copy(k_codes[1][:, h * HALF : (h + 1) * HALF], k_pool[1][:].indirect(listed))
-        for j in (0, 1, LAST_CHUNK, 2):
+            for j in range(2):
+                first_scores(j, 1, slice(h, h + 1))
+        for j in (LAST_CHUNK, 2):
             first_scores(j, 1)
         a_weights = held([P, PACK, P], F32, "a_weights")
         nc.scalar.activation(
@@ -250,22 +252,24 @@ def tile_attend_plw_proto_topk_kernel(tc, qT, k_words, k_scales, c_words, c_scal
         def weigh_first_pair(g):
             places = slice(2 * g, 2 * g + 2)
             take_best(0, 1, places)
-            take_best(1, 0, places)
-            turned = bank([P, 2, HALF], "turned_pair", 5 + g)
+            take_best(1, 1, places)
+            turned = bank([P, 2, HALF], "turned_pair", 6 + g)
             for r in range(2):
                 for j in range(2):
                     nc.tensor.transpose(turned[:, r, j * P : (j + 1) * P], best[j][:, 2 * g + r, :], identity[:])
             nc.scalar.activation(out=first_pair[:, places, :], in_=turned[:], func=ACT.Sigmoid)
             nc.sync.dma_start(y_rows[:, places, 0:HALF], first_pair[:, places, :])
 
-        def weigh(j):
-            take_best(j, 0, slice(0, PACK))
-            turned = turn(best[j], 5 + j)
-            nc.scalar.activation(out=weights[j], in_=turned[:], func=ACT.Sigmoid)
-            nc.scalar.activation(out=rounded(j), in_=turned[:].rearrange("p r q -> p q r"), func=ACT.Sigmoid)
+        def weigh_half(j, g, number):
+            places = slice(2 * g, 2 * g + 2)
+            take_best(j, 0, places)
+            turned = bank([P, 2, P], "turned_half", number)
+            for r in range(2):
+                nc.tensor.transpose(turned[:, r, :], best[j][:, 2 * g + r, :], identity[:])
+            nc.scalar.activation(out=weights[j][:, places, :], in_=turned[:], func=ACT.Sigmoid)
 
-        def round_weights(j):
-            nc.vector.tensor_copy(
+        def round_weights(j, copy):
+            copy(
                 rounded(j).rearrange("p (c i) r -> p c r i", i=LINE),
                 weights[j].rearrange("p r (c i) -> p c r i", i=LINE),
             )
@@ -276,18 +280,22 @@ def tile_attend_plw_proto_topk_kernel(tc, qT, k_words, k_scales, c_words, c_scal
                 out=y_codes[:, cols].bitcast(FP8X4), scales=y_scale[:, cols], in_=grouped[first][:].rearrange("p q r -> p (q r)")
             )
 
-        take_best(0, 0, slice(0, PACK))
+        for j in range(2):
+            take_best(j, 0, slice(0, PACK))
         weigh_first_pair(0)
         weigh_first_pair(1)
-        a_turned = turn(a_weights, 2)
-        weigh(2)
+        a_turned = turn(a_weights, 0)
+        weigh_half(2, 0, 2)
+        weigh_half(2, 1, 1)
         nc.vector.tensor_tensor(out=weights[LAST_CHUNK], in0=a_turned[:], in1=z_weights[:], op=ALU.max)
-        nc.sync.dma_start(y_rows[:, :, HALF:QUERIES], last_pair[:])
+        for g in range(2):
+            nc.sync.dma_start(y_rows[:, 2 * g : 2 * g + 2, HALF:QUERIES], last_pair[:, 2 * g : 2 * g + 2, :])
+        round_weights(2, nc.scalar.copy)
         nc.vector.tensor_copy(
             grouped[0][:].rearrange("p (c i) r -> p c r i", i=LINE),
             first_pair[:].rearrange("p r (c i) -> p c r i", i=LINE),
         )
-        round_weights(LAST_CHUNK)
+        round_weights(LAST_CHUNK, nc.vector.tensor_copy)
         hand_on(*calls[0])
         hand_on(*calls[2])
         hand_on(*calls[1])

@@ -150,10 +150,10 @@ def tile_attend_plw_proto_topk_kernel(tc, qT, k_words, k_scales, c_words, c_scal
             )
 
         pass0_low = round_queries(0, 2, 2, q_first[:, :, HALF:QUERIES], nc.scalar.copy)
-        pass0_high = round_queries(0, 0, 2, q_first[:, :, 0:HALF], nc.scalar.copy)
+        pass0_high = round_queries(0, 0, 2, q_first[:, :, 0:HALF], nc.vector.tensor_copy)
+        quantize_queries(*pass0_high)
         quantize_queries(*pass0_low)
         pass1_low = round_queries(1, 2, 2, q_second[:, :, HALF:QUERIES], nc.vector.tensor_copy)
-        quantize_queries(*pass0_high)
         pass1_high = round_queries(1, 0, 2, q_second[:, :, 0:HALF], nc.scalar.copy)
         quantize_queries(*pass1_low)
 
@@ -163,7 +163,7 @@ def tile_attend_plw_proto_topk_kernel(tc, qT, k_words, k_scales, c_words, c_scal
 
         def second_scores(j, o):
             if o == 0:
-                z_banks[j] = bank([P, SLOTS], "z_bank", (7, 7, 4, 5)[j])
+                z_banks[j] = bank([P, SLOTS], "z_bank", (7, 3, 4, 5)[j])
             scores(z_banks[j], j, o, c_codes[o][:].bitcast(FP4X4), c_scale[:, o, :])
 
         def first_scores(j, o, parts=slice(None)):
@@ -186,7 +186,7 @@ def tile_attend_plw_proto_topk_kernel(tc, qT, k_words, k_scales, c_words, c_scal
                 nc.tensor.transpose(turned[:, r, :], dealt[:, r, :], identity[:])
             return turned
 
-        for j in (3, 2, 0):
+        for j in (0, 1, 3, 2):
             second_scores(j, 0)
         quantize_queries(*pass1_high)
         for j in (3, 2):
@@ -194,17 +194,18 @@ def tile_attend_plw_proto_topk_kernel(tc, qT, k_words, k_scales, c_words, c_scal
             shift_second_scores(j)
         z_weights = held([P, PACK, P], F32, "z_weights")
         z_turned = turn(z_less_th[LAST_CHUNK], 6)
-        second_scores(0, 1)
-        shift_second_scores(0)
+        for j in range(2):
+            second_scores(j, 1)
+            shift_second_scores(j)
         nc.scalar.copy(z_weights[:], z_turned[:])
-        second_scores(1, 0)
-        second_scores(1, 1)
-        shift_second_scores(1)
         a_parts = [[(h * HALF, HALF, bank([P, HALF], "a_half", 2 * j + h)) for h in range(2)] for j in range(2)]
         a_parts.extend([(0, SLOTS, bank([P, SLOTS], "a_bank", j + 2))] for j in range(2, CHUNKS))
         nc.vector.tensor_copy(k_codes[0][:], k_pool[0][:].indirect(offsets[:]))
-        for j in range(CHUNKS):
+        first_scores(0, 0)
+        first_scores(1, 0, slice(0, 1))
+        for j in (LAST_CHUNK, 2):
             first_scores(j, 0)
+        first_scores(1, 0, slice(1, 2))
         for h in range(2):
             listed = offsets[:, h * HALF // 16 : (h + 1) * HALF // 16]
             nc.vector.tensor_copy(k_codes[1][:, h * HALF : (h + 1) * HALF], k_pool[1][:].indirect(listed))

@@ -25,9 +25,11 @@ PASS_FEATURES = P * PACK
 PASSES = FEATURES // PASS_FEATURES
 CHUNKS = QUERIES // P
 LAST_CHUNK = CHUNKS - 1
-HALF = QUERIES // 2
+PAIR = 2 * P
+HALF = SLOTS // 2
+LIST_ROWS = 16
 C_LOADED, K_LOADED = QUADRANT, P - QUADRANT
-K_PLANE = SCALE_ROWS
+K_SCALE_START = SCALE_ROWS
 FLOPS = 2 * 2 * SLOTS * FEATURES * QUERIES
 
 
@@ -43,7 +45,7 @@ def tile_attend_plw_proto_topk_kernel(tc, qT, k_words, k_scales, c_words, c_scal
         def held(shape, dtype, name, tag=None):
             return keep.tile(shape, dtype, name=name, tag=tag or name, align_bytes=64)
 
-        offsets = held([P, SLOTS // 16], U16, "offsets")
+        offsets = held([P, SLOTS // LIST_ROWS], U16, "offsets")
         c_pool = held([P, TOKENS], U32, "c_pool", "first_pool")
         c_scale_pool = held([P, TOKENS], U8, "c_scale_pool", "second_queries")
         k_scale_pool = held([P, TOKENS], U8, "k_scale_pool", "third_pool")
@@ -53,9 +55,9 @@ def tile_attend_plw_proto_topk_kernel(tc, qT, k_words, k_scales, c_words, c_scal
         identity = held([P, P], F32, "identity")
         warm = held([P, 16], F32, "warm")
 
-        def load_queries(o, first, chunks, tag):
-            raw = held([P, PACK, chunks * P], F32, "q_raw%d%d" % (o, first), tag)
-            rows = qT[0, PASS_FEATURES * o : PASS_FEATURES * (o + 1), first * P : (first + chunks) * P]
+        def load_queries(o, tag):
+            raw = held([P, PACK, QUERIES], F32, "q_raw%d" % o, tag)
+            rows = qT[0, PASS_FEATURES * o : PASS_FEATURES * (o + 1), :]
             nc.sync.dma_start(raw[:], rows.rearrange("(p j) w -> p j w", j=PACK))
             return raw
 
@@ -74,7 +76,7 @@ def tile_attend_plw_proto_topk_kernel(tc, qT, k_words, k_scales, c_words, c_scal
                 pool[loaded : loaded + QUADRANT, :].bitcast(I32), scales.rearrange("o f t -> f o t").bitcast(I32)
             )
         nc.sync.dma_start(c_pool[:].bitcast(I32), c_words[0].rearrange("p t b -> p (t b)").bitcast(I32))
-        q_first = load_queries(0, 0, CHUNKS, "first_queries")
+        q_first = load_queries(0, "first_queries")
         nc.scalar.dma_start(th_rows[0:CHUNKS, :], th[0, 0].rearrange("(j p) -> j p", p=P))
         nc.scalar.activation(out=warm[:, 8:9], in_=warm[:, 0:1], func=ACT.Sigmoid)
 
@@ -92,7 +94,7 @@ def tile_attend_plw_proto_topk_kernel(tc, qT, k_words, k_scales, c_words, c_scal
                 )
 
         move_scales(gather_scales(c_scale_pool, "c_scale_listed"), C_LOADED, c_scale, 0)
-        q_second = load_queries(1, 0, CHUNKS, "second_queries")
+        q_second = load_queries(1, "second_queries")
         k_scale_listed = gather_scales(k_scale_pool, "k_scale_listed")
 
         k_pool = []
@@ -102,7 +104,7 @@ def tile_attend_plw_proto_topk_kernel(tc, qT, k_words, k_scales, c_words, c_scal
             nc.sync.dma_start(k_pool[o][:].bitcast(I32), k_words[o].rearrange("p t b -> p (t b)").bitcast(I32))
 
         load_first_keys(0, "third_pool")
-        move_scales(k_scale_listed, K_LOADED, k_scale, K_PLANE)
+        move_scales(k_scale_listed, K_LOADED, k_scale, K_SCALE_START)
 
         c_listed = held([P, SLOTS], U32, "c_listed")
         nc.vector.tensor_copy(c_listed[:], c_pool[:].indirect(offsets[:]))
@@ -119,24 +121,24 @@ def tile_attend_plw_proto_topk_kernel(tc, qT, k_words, k_scales, c_words, c_scal
 
         q_codes = {}
         q_scale = {}
+        q_rounded = {}
 
-        def round_queries(o, first, chunks, raw, copy):
-            grouped = held([P, chunks * P, PACK], BF16, "q_grouped%d%d" % (o, first))
+        def round_queries(o, pair, raw, copy):
+            q_rounded[o, pair] = held([P, PAIR, PACK], BF16, "q_rounded%d%d" % (o, pair))
             copy(
-                grouped[:].rearrange("p (c i) t -> p c t i", i=LINE),
-                raw.rearrange("p t (c i) -> p c t i", i=LINE),
+                q_rounded[o, pair][:].rearrange("p (c i) t -> p c t i", i=LINE),
+                raw[:, :, pair * PAIR : (pair + 1) * PAIR].rearrange("p t (c i) -> p c t i", i=LINE),
             )
-            return o, first, chunks, grouped
 
-        def quantize_queries(o, first, chunks, grouped):
-            codes = held([P, chunks * P], U32, "q_codes%d%d" % (o, first))
-            scale = held([P, chunks * P], U8, "q_scale%d%d" % (o, first))
+        def quantize_queries(o, pair):
+            codes = held([P, PAIR], U32, "q_codes%d%d" % (o, pair))
+            scale = held([P, PAIR], U8, "q_scale%d%d" % (o, pair))
             nc.vector.quantize_mx(
-                out=codes[:].bitcast(FP8X4), scales=scale[:], in_=grouped[:].rearrange("p w t -> p (w t)")
+                out=codes[:].bitcast(FP8X4), scales=scale[:], in_=q_rounded[o, pair][:].rearrange("p w t -> p (w t)")
             )
-            for c in range(chunks):
-                q_codes[o, first + c] = codes[:, c * P : (c + 1) * P]
-                q_scale[o, first + c] = scale[:, c * P : (c + 1) * P]
+            for c in range(2):
+                q_codes[o, 2 * pair + c] = codes[:, c * P : (c + 1) * P]
+                q_scale[o, 2 * pair + c] = scale[:, c * P : (c + 1) * P]
 
         def scores(sums, j, o, codes, scale):
             nc.tensor.matmul_mx(
@@ -149,32 +151,33 @@ def tile_attend_plw_proto_topk_kernel(tc, qT, k_words, k_scales, c_words, c_scal
                 stop=(o == PASSES - 1),
             )
 
-        pass0_low = round_queries(0, 2, 2, q_first[:, :, HALF:QUERIES], nc.scalar.copy)
-        pass0_high = round_queries(0, 0, 2, q_first[:, :, 0:HALF], nc.vector.tensor_copy)
-        quantize_queries(*pass0_high)
-        quantize_queries(*pass0_low)
-        pass1_low = round_queries(1, 2, 2, q_second[:, :, HALF:QUERIES], nc.vector.tensor_copy)
-        pass1_high = round_queries(1, 0, 2, q_second[:, :, 0:HALF], nc.scalar.copy)
-        quantize_queries(*pass1_low)
+        round_queries(0, 1, q_first, nc.scalar.copy)
+        round_queries(0, 0, q_first, nc.vector.tensor_copy)
+        quantize_queries(0, 0)
+        quantize_queries(0, 1)
+        round_queries(1, 1, q_second, nc.vector.tensor_copy)
+        round_queries(1, 0, q_second, nc.scalar.copy)
+        quantize_queries(1, 1)
 
+        z_bank_numbers = (3, 7, 4, 5)
         k_codes = [held([P, SLOTS], U32, "k_codes%d" % o) for o in range(PASSES)]
         z_banks = {}
-        z_less_th = {}
+        z_dealt = {}
 
         def second_scores(j, o):
             if o == 0:
-                z_banks[j] = bank([P, SLOTS], "z_bank", (7, 3, 4, 5)[j])
+                z_banks[j] = bank([P, SLOTS], "z_bank", z_bank_numbers[j])
             scores(z_banks[j], j, o, c_codes[o][:].bitcast(FP4X4), c_scale[:, o, :])
 
         def first_scores(j, o, parts=slice(None)):
-            for first, count, part in a_parts[j][parts]:
-                cols = slice(first, first + count)
-                scores(part, j, o, k_codes[o][:, cols].bitcast(FP8X4), k_scale[K_PLANE:P, o, cols])
+            for first_slot, slots, part in a_parts[j][parts]:
+                cols = slice(first_slot, first_slot + slots)
+                scores(part, j, o, k_codes[o][:, cols].bitcast(FP8X4), k_scale[K_SCALE_START:P, o, cols])
 
-        def shift_second_scores(j):
-            z_less_th[j] = held([P, PACK, P], F32, "z_less_th%d" % j)
+        def deal_second_scores(j):
+            z_dealt[j] = held([P, PACK, P], F32, "z_dealt%d" % j)
             nc.scalar.activation(
-                out=z_less_th[j][:],
+                out=z_dealt[j][:],
                 in_=z_banks[j][:].rearrange("p (s r) -> p r s", r=PACK),
                 func=ACT.Sigmoid if j == LAST_CHUNK else ACT.Identity,
                 bias=minus_th[:, j : j + 1],
@@ -186,17 +189,17 @@ def tile_attend_plw_proto_topk_kernel(tc, qT, k_words, k_scales, c_words, c_scal
                 nc.tensor.transpose(turned[:, r, :], dealt[:, r, :], identity[:])
             return turned
 
-        for j in (0, 1, 3, 2):
+        for j in (0, 1, LAST_CHUNK, 2):
             second_scores(j, 0)
-        quantize_queries(*pass1_high)
-        for j in (3, 2):
+        quantize_queries(1, 0)
+        for j in (LAST_CHUNK, 2):
             second_scores(j, 1)
-            shift_second_scores(j)
+            deal_second_scores(j)
         z_weights = held([P, PACK, P], F32, "z_weights")
-        z_turned = turn(z_less_th[LAST_CHUNK], 6)
+        z_turned = turn(z_dealt[LAST_CHUNK], 6)
         for j in range(2):
             second_scores(j, 1)
-            shift_second_scores(j)
+            deal_second_scores(j)
         nc.scalar.copy(z_weights[:], z_turned[:])
         a_parts = [[(h * HALF, HALF, bank([P, HALF], "a_half", 2 * j + h)) for h in range(2)] for j in range(2)]
         a_parts.extend([(0, SLOTS, bank([P, SLOTS], "a_bank", j + 2))] for j in range(2, CHUNKS))
@@ -207,7 +210,7 @@ def tile_attend_plw_proto_topk_kernel(tc, qT, k_words, k_scales, c_words, c_scal
             first_scores(j, 0)
         first_scores(1, 0, slice(1, 2))
         for h in range(2):
-            listed = offsets[:, h * HALF // 16 : (h + 1) * HALF // 16]
+            listed = offsets[:, h * HALF // LIST_ROWS : (h + 1) * HALF // LIST_ROWS]
             nc.vector.tensor_copy(k_codes[1][:, h * HALF : (h + 1) * HALF], k_pool[1][:].indirect(listed))
             for j in range(2):
                 first_scores(j, 1, slice(h, h + 1))
@@ -225,81 +228,76 @@ def tile_attend_plw_proto_topk_kernel(tc, qT, k_words, k_scales, c_words, c_scal
         y_scale = held([P, QUERIES], U8, "y_scale")
         y_rows = out_0.rearrange("(p r) q -> p r q", r=PACK)
         word_rows = out_1[0].rearrange("p q b -> p (q b)").bitcast(I32)
-        last_pair = held([P, PACK, HALF], F32, "last_pair")
-        first_pair = held([P, PACK, HALF], F32, "first_pair")
-        weights = [first_pair[:, :, 0:P], first_pair[:, :, P:HALF]]
-        weights.extend([last_pair[:, :, 0:P], last_pair[:, :, P:HALF]])
+        last_pair = held([P, PACK, PAIR], F32, "last_pair")
+        first_pair = held([P, PACK, PAIR], F32, "first_pair")
+        weights2, weights3 = last_pair[:, :, 0:P], last_pair[:, :, P:PAIR]
 
-        calls = ((0, 2), (2, 1), (3, 1))
-        grouped = {first: held([P, count * P, PACK], BF16, "y_grouped%d" % first) for first, count in calls}
-
-        def rounded(j):
-            return grouped[0][:, j * P : (j + 1) * P, :] if j < 2 else grouped[j][:]
-
+        y_chunks = {0: 2, 2: 1, LAST_CHUNK: 1}
+        y_rounded = {j: held([P, y_chunks[j] * P, PACK], BF16, "y_rounded%d" % j) for j in y_chunks}
         best = [held([P, PACK, P], F32, "best%d" % j) for j in range(LAST_CHUNK)]
 
-        def take_best(j, number, places):
-            first, count, part = a_parts[j][number]
-            rows = slice(first // PACK, (first + count) // PACK)
+        def take_best(j, which, places):
+            first_slot, slots, part = a_parts[j][which]
+            rows = slice(first_slot // PACK, (first_slot + slots) // PACK)
             nc.vector.scalar_tensor_tensor(
                 out=best[j][:, places, rows],
                 in0=part[:].rearrange("p (s r) -> p r s", r=PACK)[:, places, :],
                 scalar=minus_th[:, j : j + 1],
-                in1=z_less_th[j][:, places, rows],
+                in1=z_dealt[j][:, places, rows],
                 op0=ALU.add,
                 op1=ALU.max,
             )
 
-        def weigh_first_pair(g):
-            places = slice(2 * g, 2 * g + 2)
+        def weigh_first_pair(place, count, number):
+            places = slice(place, place + count)
             take_best(0, 1, places)
             take_best(1, 1, places)
-            turned = bank([P, 2, HALF], "turned_pair", 6 + g)
-            for r in range(2):
+            turned = bank([P, count, PAIR], "turned_pair", number)
+            for r in range(count):
                 for j in range(2):
-                    nc.tensor.transpose(turned[:, r, j * P : (j + 1) * P], best[j][:, 2 * g + r, :], identity[:])
+                    nc.tensor.transpose(turned[:, r, j * P : (j + 1) * P], best[j][:, place + r, :], identity[:])
             nc.scalar.activation(out=first_pair[:, places, :], in_=turned[:], func=ACT.Sigmoid)
-            nc.sync.dma_start(y_rows[:, places, 0:HALF], first_pair[:, places, :])
+            nc.sync.dma_start(y_rows[:, places, 0:PAIR], first_pair[:, places, :])
 
-        def weigh_half(j, g, number):
-            places = slice(2 * g, 2 * g + 2)
-            take_best(j, 0, places)
-            turned = bank([P, 2, P], "turned_half", number)
+        def weigh_chunk_2(place, number):
+            places = slice(place, place + 2)
+            take_best(2, 0, places)
+            turned = bank([P, 2, P], "turned_places", number)
             for r in range(2):
-                nc.tensor.transpose(turned[:, r, :], best[j][:, 2 * g + r, :], identity[:])
-            nc.scalar.activation(out=weights[j][:, places, :], in_=turned[:], func=ACT.Sigmoid)
+                nc.tensor.transpose(turned[:, r, :], best[2][:, place + r, :], identity[:])
+            nc.scalar.activation(out=weights2[:, places, :], in_=turned[:], func=ACT.Sigmoid)
 
-        def round_weights(j, copy):
+        def round_weights(j, weights, copy):
             copy(
-                rounded(j).rearrange("p (c i) r -> p c r i", i=LINE),
-                weights[j].rearrange("p r (c i) -> p c r i", i=LINE),
+                y_rounded[j][:].rearrange("p (c i) r -> p c r i", i=LINE),
+                weights.rearrange("p r (c i) -> p c r i", i=LINE),
             )
 
-        def hand_on(first, count):
-            cols = slice(first * P, (first + count) * P)
+        def hand_on(j):
+            cols = slice(j * P, (j + y_chunks[j]) * P)
             nc.vector.quantize_mx(
-                out=y_codes[:, cols].bitcast(FP8X4), scales=y_scale[:, cols], in_=grouped[first][:].rearrange("p q r -> p (q r)")
+                out=y_codes[:, cols].bitcast(FP8X4),
+                scales=y_scale[:, cols],
+                in_=y_rounded[j][:].rearrange("p q r -> p (q r)"),
             )
 
         for j in range(2):
             take_best(j, 0, slice(0, PACK))
-        weigh_first_pair(0)
-        weigh_first_pair(1)
-        a_turned = turn(a_weights, 0)
-        weigh_half(2, 0, 2)
-        weigh_half(2, 1, 1)
-        nc.vector.tensor_tensor(out=weights[LAST_CHUNK], in0=a_turned[:], in1=z_weights[:], op=ALU.max)
-        for g in range(2):
-            nc.sync.dma_start(y_rows[:, 2 * g : 2 * g + 2, HALF:QUERIES], last_pair[:, 2 * g : 2 * g + 2, :])
-        round_weights(2, nc.scalar.copy)
-        nc.vector.tensor_copy(
-            grouped[0][:].rearrange("p (c i) r -> p c r i", i=LINE),
-            first_pair[:].rearrange("p r (c i) -> p c r i", i=LINE),
-        )
-        round_weights(LAST_CHUNK, nc.vector.tensor_copy)
-        hand_on(*calls[0])
-        hand_on(*calls[2])
-        hand_on(*calls[1])
+        weigh_first_pair(0, 1, 6)
+        weigh_first_pair(1, 1, 7)
+        weigh_first_pair(2, 2, 0)
+        a_turned = turn(a_weights, 2)
+        weigh_chunk_2(0, 1)
+        weigh_chunk_2(2, 3)
+        nc.vector.tensor_tensor(out=weights3, in0=a_turned[:], in1=z_weights[:], op=ALU.max)
+        for place in (0, 2):
+            nc.sync.dma_start(y_rows[:, place : place + 2, PAIR:QUERIES], last_pair[:, place : place + 2, :])
+
+        round_weights(LAST_CHUNK, weights3, nc.scalar.copy)
+        round_weights(0, first_pair[:], nc.vector.tensor_copy)
+        round_weights(2, weights2, nc.vector.tensor_copy)
+        for j in (0, LAST_CHUNK, 2):
+            hand_on(j)
         nc.sync.dma_start(word_rows, y_codes[:].bitcast(I32))
         for quad in range(QUADRANTS):
             nc.scalar.dma_start(

@@ -43,7 +43,7 @@ def tile_attend_plw_proto_topk_kernel(tc, qT, k_words, k_scales, c_words, c_scal
             return psum.tile(shape, F32, name=name, tag="bank%d" % number)
 
         def held(shape, dtype, name, tag=None):
-            return keep.tile(shape, dtype, name=name, tag=tag or name, align_bytes=64)
+            return keep.tile(shape, dtype, name=name, tag=tag or name, align_bytes=256)
 
         offsets = held([P, SLOTS // LIST_ROWS], U16, "offsets")
         c_pool = held([P, TOKENS], U32, "c_pool", "first_pool")

@@ -28,7 +28,7 @@ LAST_CHUNK = CHUNKS - 1
 PAIR = 2 * P
 HALF = SLOTS // 2
 LIST_ROWS = 16
-C_LOADED, K_LOADED = QUADRANT, P - QUADRANT
+C_LOADED = K_LOADED = P - QUADRANT
 K_SCALE_START = SCALE_ROWS
 FLOPS = 2 * 2 * SLOTS * FEATURES * QUERIES
 
@@ -49,8 +49,8 @@ def tile_attend_plw_proto_topk_kernel(tc, qT, k_words, k_scales, c_words, c_scal
         c_pool = held([P, TOKENS], U32, "c_pool", "first_pool")
         c_scale_pool = held([P, TOKENS], U8, "c_scale_pool", "second_queries")
         k_scale_pool = held([P, TOKENS], U8, "k_scale_pool", "third_pool")
-        c_scale = held([P, PASSES, SLOTS], U8, "c_scale")
-        k_scale = held([P, PASSES, SLOTS], U8, "k_scale")
+        planes = held([P, 2, PASSES, SLOTS], U8, "planes")
+        c_scale, k_scale = planes[:, 0], planes[:, 1]
         th_rows = held([P, P], F32, "th_rows")
         identity = held([P, P], F32, "identity")
         warm = held([P, 16], F32, "warm")
@@ -63,10 +63,8 @@ def tile_attend_plw_proto_topk_kernel(tc, qT, k_words, k_scales, c_words, c_scal
 
         nc.vector.memset(warm[:, 0:1], 0.0)
         nc.vector.memset(c_scale_pool[0:C_LOADED, :].bitcast(I32), 0)
-        nc.vector.memset(c_scale_pool[C_LOADED + QUADRANT : P, :].bitcast(I32), 0)
         nc.vector.memset(k_scale_pool[0:K_LOADED, :].bitcast(I32), 0)
-        for plane in (c_scale, k_scale):
-            nc.vector.memset(plane[:].rearrange("p o n -> p (o n)").bitcast(I32), 0)
+        nc.vector.memset(planes[:].rearrange("p s o n -> p (s o n)").bitcast(I32), 0)
         nc.gpsimd.memset(th_rows[:], 0.0)
         make_identity(nc, identity[:])
 
@@ -108,10 +106,8 @@ def tile_attend_plw_proto_topk_kernel(tc, qT, k_words, k_scales, c_words, c_scal
 
         c_listed = held([P, SLOTS], U32, "c_listed")
         nc.vector.tensor_copy(c_listed[:], c_pool[:].indirect(offsets[:]))
-        c_codes = [held([P, 2 * SLOTS], U8, "c_codes%d" % o) for o in range(PASSES)]
-        c_halves = c_listed[:].bitcast(U16).rearrange("p (n h) -> p h n", h=PASSES)
-        for o in range(PASSES):
-            nc.vector.tensor_copy(c_codes[o][:].bitcast(U16), c_halves[:, o, :])
+        c_codes = held([P, PASSES, 2 * SLOTS], U8, "c_codes")
+        nc.vector.tensor_copy(c_codes[:].bitcast(U16), c_listed[:].bitcast(U16).rearrange("p (n h) -> p h n", h=PASSES))
         load_first_keys(1, "first_pool")
 
         th_turned = bank([P, P], "th_turned", 1)
@@ -167,7 +163,7 @@ def tile_attend_plw_proto_topk_kernel(tc, qT, k_words, k_scales, c_words, c_scal
         def second_scores(j, o):
             if o == 0:
                 z_banks[j] = bank([P, SLOTS], "z_bank", z_bank_numbers[j])
-            scores(z_banks[j], j, o, c_codes[o][:].bitcast(FP4X4), c_scale[:, o, :])
+            scores(z_banks[j], j, o, c_codes[:, o, :].bitcast(FP4X4), c_scale[:, o, :])
 
         def first_scores(j, o, parts=slice(None)):
             for first_slot, slots, part in a_parts[j][parts]:

@@ -286,17 +286,18 @@ def tile_attend_plw_proto_topk_kernel(tc, qT, k_words, k_scales, c_words, c_scal
         weigh_chunk_2(0, 1)
         weigh_chunk_2(2, 3)
         nc.vector.tensor_tensor(out=weights3, in0=a_turned[:], in1=z_weights[:], op=ALU.max)
-        for place in (0, 2):
-            nc.sync.dma_start(y_rows[:, place : place + 2, PAIR:QUERIES], last_pair[:, place : place + 2, :])
+        nc.sync.dma_start(y_rows[:, :, PAIR:QUERIES], last_pair[:])
 
         round_weights(LAST_CHUNK, weights3, nc.scalar.copy)
         round_weights(0, first_pair[:], nc.vector.tensor_copy)
         round_weights(2, weights2, nc.vector.tensor_copy)
-        for j in (0, LAST_CHUNK, 2):
+        hand_on(0)
+        nc.sync.dma_start(word_rows[:, 0:PAIR], y_codes[:, 0:PAIR].bitcast(I32))
+        for j in (LAST_CHUNK, 2):
             hand_on(j)
-        nc.sync.dma_start(word_rows, y_codes[:].bitcast(I32))
+        nc.sync.dma_start(word_rows[:, PAIR:QUERIES], y_codes[:, PAIR:QUERIES].bitcast(I32))
         for quad in range(QUADRANTS):
-            nc.scalar.dma_start(
+            (nc.scalar, nc.sync)[quad % 2].dma_start(
                 out_2[0, SCALE_ROWS * quad : SCALE_ROWS * (quad + 1), :].bitcast(I32),
                 y_scale[QUADRANT * quad : QUADRANT * quad + SCALE_ROWS, :].bitcast(I32),
             )

@@ -197,28 +197,29 @@ def tile_attend_plw_proto_topk_kernel(tc, qT, k_words, k_scales, c_words, c_scal
             second_scores(j, 1)
             deal_second_scores(j)
         nc.scalar.copy(z_weights[:], z_turned[:])
-        a_parts = [[(h * HALF, HALF, bank([P, HALF], "a_half", 2 * j + h)) for h in range(2)] for j in range(2)]
-        a_parts.extend([(0, SLOTS, bank([P, SLOTS], "a_bank", j + 2))] for j in range(2, CHUNKS))
+        halves = {0: (0, 1), 1: (2, 3), LAST_CHUNK: (5, 7)}
+        a_parts = {j: [(h * HALF, HALF, bank([P, HALF], "a_half", n)) for h, n in enumerate(halves[j])] for j in halves}
+        a_parts[2] = [(0, SLOTS, bank([P, SLOTS], "a_bank", 4))]
         nc.vector.tensor_copy(k_codes[0][:], k_pool[0][:].indirect(offsets[:]))
         first_scores(0, 0)
         first_scores(1, 0, slice(0, 1))
-        for j in (LAST_CHUNK, 2):
-            first_scores(j, 0)
+        first_scores(LAST_CHUNK, 0, slice(0, 1))
+        first_scores(2, 0)
         first_scores(1, 0, slice(1, 2))
+        first_scores(LAST_CHUNK, 0, slice(1, 2))
+        a_weights = held([P, PACK, P], F32, "a_weights")
         for h in range(2):
             listed = offsets[:, h * HALF // LIST_ROWS : (h + 1) * HALF // LIST_ROWS]
             nc.vector.tensor_copy(k_codes[1][:, h * HALF : (h + 1) * HALF], k_pool[1][:].indirect(listed))
-            for j in range(2):
+            for j in halves:
                 first_scores(j, 1, slice(h, h + 1))
-        for j in (LAST_CHUNK, 2):
-            first_scores(j, 1)
-        a_weights = held([P, PACK, P], F32, "a_weights")
-        nc.scalar.activation(
-            out=a_weights[:],
-            in_=a_parts[LAST_CHUNK][0][2][:].rearrange("p (s r) -> p r s", r=PACK),
-            func=ACT.Sigmoid,
-            bias=minus_th[:, LAST_CHUNK : LAST_CHUNK + 1],
-        )
+            nc.scalar.activation(
+                out=a_weights[:, :, h * HALF // PACK : (h + 1) * HALF // PACK],
+                in_=a_parts[LAST_CHUNK][h][2][:].rearrange("p (s r) -> p r s", r=PACK),
+                func=ACT.Sigmoid,
+                bias=minus_th[:, LAST_CHUNK : LAST_CHUNK + 1],
+            )
+        first_scores(2, 1)
 
         y_codes = held([P, QUERIES], U32, "y_codes")
         y_scale = held([P, QUERIES], U8, "y_scale")
@@ -229,7 +230,6 @@ def tile_attend_plw_proto_topk_kernel(tc, qT, k_words, k_scales, c_words, c_scal
         weights2, weights3 = last_pair[:, :, 0:P], last_pair[:, :, P:PAIR]
 
         y_chunks = {0: 2, 2: 1, LAST_CHUNK: 1}
-        y_rounded = {j: held([P, y_chunks[j] * P, PACK], BF16, "y_rounded%d" % j) for j in y_chunks}
         best = [held([P, PACK, P], F32, "best%d" % j) for j in range(LAST_CHUNK)]
 
         def take_best(j, which, places):
@@ -244,16 +244,12 @@ def tile_attend_plw_proto_topk_kernel(tc, qT, k_words, k_scales, c_words, c_scal
                 op1=ALU.max,
             )
 
-        def weigh_first_pair(place, count, number):
-            places = slice(place, place + count)
-            take_best(0, 1, places)
-            take_best(1, 1, places)
-            turned = bank([P, count, PAIR], "turned_pair", number)
-            for r in range(count):
-                for j in range(2):
-                    nc.tensor.transpose(turned[:, r, j * P : (j + 1) * P], best[j][:, place + r, :], identity[:])
-            nc.scalar.activation(out=first_pair[:, places, :], in_=turned[:], func=ACT.Sigmoid)
-            nc.sync.dma_start(y_rows[:, places, 0:PAIR], first_pair[:, places, :])
+        def weigh_first_pair(place, number):
+            turned = bank([P, PAIR], "turned_pair", number)
+            for j in range(2):
+                nc.tensor.transpose(turned[:, j * P : (j + 1) * P], best[j][:, place, :], identity[:])
+            nc.scalar.activation(out=first_pair[:, place, :], in_=turned[:], func=ACT.Sigmoid)
+            nc.sync.dma_start(y_rows[:, place, 0:PAIR], first_pair[:, place, :])
 
         def weigh_chunk_2(place, number):
             places = slice(place, place + 2)
@@ -279,15 +275,20 @@ def tile_attend_plw_proto_topk_kernel(tc, qT, k_words, k_scales, c_words, c_scal
 
         for j in range(2):
             take_best(j, 0, slice(0, PACK))
-        weigh_first_pair(0, 1, 6)
-        weigh_first_pair(1, 1, 7)
-        weigh_first_pair(2, 2, 0)
-        a_turned = turn(a_weights, 2)
-        weigh_chunk_2(0, 1)
+        for places in (slice(0, 1), slice(1, 2), slice(2, PACK)):
+            for j in range(2):
+                take_best(j, 1, places)
+        for place, number in enumerate((6, 5, 0, 2)):
+            weigh_first_pair(place, number)
+        a_turned = turn(a_weights, 1)
+        weigh_chunk_2(0, 7)
         weigh_chunk_2(2, 3)
         nc.vector.tensor_tensor(out=weights3, in0=a_turned[:], in1=z_weights[:], op=ALU.max)
-        nc.sync.dma_start(y_rows[:, :, PAIR:QUERIES], last_pair[:])
+        for place in (0, 2):
+            nc.sync.dma_start(y_rows[:, place : place + 2, PAIR:QUERIES], last_pair[:, place : place + 2, :])
 
+        y_tags = {0: "a_weights", 2: None, LAST_CHUNK: "best2"}
+        y_rounded = {j: held([P, y_chunks[j] * P, PACK], BF16, "y_rounded%d" % j, y_tags[j]) for j in y_chunks}
         round_weights(LAST_CHUNK, weights3, nc.scalar.copy)
         round_weights(0, first_pair[:], nc.vector.tensor_copy)
         round_weights(2, weights2, nc.vector.tensor_copy)

@@ -47,8 +47,8 @@ def tile_attend_plw_proto_topk_kernel(tc, qT, k_words, k_scales, c_words, c_scal
 
         offsets = held([P, SLOTS // LIST_ROWS], U16, "offsets")
         c_pool = held([P, TOKENS], U32, "c_pool", "first_pool")
-        c_scale_pool = held([P, TOKENS], U8, "c_scale_pool", "second_queries")
-        k_scale_pool = held([P, TOKENS], U8, "k_scale_pool", "third_pool")
+        c_scale_pool = held([P, TOKENS], U8, "c_scale_pool")
+        k_scale_pool = held([P, TOKENS], U8, "k_scale_pool", "second_queries")
         planes = held([P, 2, PASSES, SLOTS], U8, "planes")
         c_scale, k_scale = planes[:, 0], planes[:, 1]
         th_rows = held([P, P], F32, "th_rows")
@@ -86,14 +86,15 @@ def tile_attend_plw_proto_topk_kernel(tc, qT, k_words, k_scales, c_words, c_scal
         def move_scales(listed, loaded, plane, start):
             rows = SCALE_ROWS * PASSES
             for quad in range(QUADRANTS):
-                nc.sync.dma_start(
+                nc.scalar.dma_start(
                     plane[QUADRANT * quad + start : QUADRANT * quad + start + SCALE_ROWS].bitcast(I32),
                     listed[loaded + rows * quad : loaded + rows * (quad + 1), :].bitcast(I32),
                 )
 
         move_scales(gather_scales(c_scale_pool, "c_scale_listed"), C_LOADED, c_scale, 0)
-        q_second = load_queries(1, "second_queries")
         k_scale_listed = gather_scales(k_scale_pool, "k_scale_listed")
+        q_second = load_queries(1, "second_queries")
+        move_scales(k_scale_listed, K_LOADED, k_scale, K_SCALE_START)
 
         k_pool = []
 
@@ -101,14 +102,12 @@ def tile_attend_plw_proto_topk_kernel(tc, qT, k_words, k_scales, c_words, c_scal
             k_pool.append(held([P, TOKENS], U32, "k_pool%d" % o, tag))
             nc.sync.dma_start(k_pool[o][:].bitcast(I32), k_words[o].rearrange("p t b -> p (t b)").bitcast(I32))
 
-        load_first_keys(0, "third_pool")
-        move_scales(k_scale_listed, K_LOADED, k_scale, K_SCALE_START)
 
         c_listed = held([P, SLOTS], U32, "c_listed")
         nc.vector.tensor_copy(c_listed[:], c_pool[:].indirect(offsets[:]))
         c_codes = held([P, PASSES, 2 * SLOTS], U8, "c_codes")
         nc.vector.tensor_copy(c_codes[:].bitcast(U16), c_listed[:].bitcast(U16).rearrange("p (n h) -> p h n", h=PASSES))
-        load_first_keys(1, "first_pool")
+        load_first_keys(0, "first_pool")
 
         th_turned = bank([P, P], "th_turned", 1)
         nc.tensor.transpose(th_turned[:], th_rows[:], identity[:])
@@ -151,6 +150,7 @@ def tile_attend_plw_proto_topk_kernel(tc, qT, k_words, k_scales, c_words, c_scal
         round_queries(0, 0, q_first, nc.vector.tensor_copy)
         quantize_queries(0, 0)
         quantize_queries(0, 1)
+        load_first_keys(1, "first_queries")
         round_queries(1, 1, q_second, nc.vector.tensor_copy)
         round_queries(1, 0, q_second, nc.scalar.copy)
         quantize_queries(1, 1)

from contextlib import ExitStack

import concourse.mybir as mybir
from concourse.masks import make_identity

F32 = mybir.dt.float32
BF16 = mybir.dt.bfloat16
I32 = mybir.dt.int32
U32 = mybir.dt.uint32
U16 = mybir.dt.uint16
U8 = mybir.dt.uint8
FP8X4 = mybir.dt.float8_e4m3fn_x4
FP4X4 = mybir.dt.float4_e2m1fn_x4
ALU = mybir.AluOpType
ACT = mybir.ActivationFunctionType

P = 128
PACK = 4
QUADRANT = 32
QUADRANTS = P // QUADRANT
SCALE_ROWS = 4
LINE = 4
SLOTS, TOKENS, FEATURES, QUERIES = 512, 2048, 1024, 512
PASS_FEATURES = P * PACK
PASSES = FEATURES // PASS_FEATURES
CHUNKS = QUERIES // P
LAST_CHUNK = CHUNKS - 1
PAIR = 2 * P
HALF = SLOTS // 2
LIST_ROWS = 16
C_LOADED = K_LOADED = P - QUADRANT
K_SCALE_START = SCALE_ROWS
FLOPS = 2 * 2 * SLOTS * FEATURES * QUERIES


def tile_attend_plw_proto_topk_kernel(tc, qT, k_words, k_scales, c_words, c_scales, th, offs, out_0, out_1, out_2):
    nc = tc.nc
    with ExitStack() as ctx:
        keep = ctx.enter_context(tc.tile_pool(name="keep", bufs=1))
        psum = ctx.enter_context(tc.psum_pool(name="psum", bufs=1))

        def bank(shape, name, number):
            return psum.tile(shape, F32, name=name, tag="bank%d" % number)

        def held(shape, dtype, name, tag=None):
            return keep.tile(shape, dtype, name=name, tag=tag or name, align_bytes=256)

        offsets = held([P, SLOTS // LIST_ROWS], U16, "offsets")
        c_pool = held([P, TOKENS], U32, "c_pool", "first_pool")
        c_scale_pool = held([P, TOKENS], U8, "c_scale_pool")
        k_scale_pool = held([P, TOKENS], U8, "k_scale_pool", "second_queries")
        planes = held([P, 2, PASSES, SLOTS], U8, "planes")
        c_scale, k_scale = planes[:, 0], planes[:, 1]
        th_rows = held([P, P], F32, "th_rows")
        identity = held([P, P], F32, "identity")
        warm = held([P, 16], F32, "warm")

        def load_queries(o, tag):
            raw = held([P, PACK, QUERIES], F32, "q_raw%d" % o, tag)
            rows = qT[0, PASS_FEATURES * o : PASS_FEATURES * (o + 1), :]
            nc.sync.dma_start(raw[:], rows.rearrange("(p j) w -> p j w", j=PACK))
            return raw

        nc.vector.memset(warm[:, 0:1], 0.0)
        nc.vector.memset(c_scale_pool[0:C_LOADED, :].bitcast(I32), 0)
        nc.vector.memset(k_scale_pool[0:K_LOADED, :].bitcast(I32), 0)
        nc.vector.memset(planes[:].rearrange("p s o n -> p (s o n)").bitcast(I32), 0)
        nc.gpsimd.memset(th_rows[:], 0.0)
        make_identity(nc, identity[:])

        nc.sync.dma_start(offsets[:], offs)
        for pool, scales, loaded in ((c_scale_pool, c_scales, C_LOADED), (k_scale_pool, k_scales, K_LOADED)):
            nc.sync.dma_start(
                pool[loaded : loaded + QUADRANT, :].bitcast(I32), scales.rearrange("o f t -> f o t").bitcast(I32)
            )
        nc.sync.dma_start(c_pool[:].bitcast(I32), c_words[0].rearrange("p t b -> p (t b)").bitcast(I32))
        q_first = load_queries(0, "first_queries")
        nc.scalar.dma_start(th_rows[0:CHUNKS, :], th[0, 0].rearrange("(j p) -> j p", p=P))
        nc.scalar.activation(out=warm[:, 8:9], in_=warm[:, 0:1], func=ACT.Sigmoid)

        def gather_scales(pool, name):
            listed = held([P, SLOTS], U8, name)
            nc.vector.tensor_copy(listed[:], pool[:].indirect(offsets[:]))
            return listed

        def move_scales(listed, loaded, plane, start):
            rows = SCALE_ROWS * PASSES
            for quad in range(QUADRANTS):
                nc.scalar.dma_start(
                    plane[QUADRANT * quad + start : QUADRANT * quad + start + SCALE_ROWS].bitcast(I32),
                    listed[loaded + rows * quad : loaded + rows * (quad + 1), :].bitcast(I32),
                )

        move_scales(gather_scales(c_scale_pool, "c_scale_listed"), C_LOADED, c_scale, 0)
        k_scale_listed = gather_scales(k_scale_pool, "k_scale_listed")
        q_second = load_queries(1, "second_queries")
        move_scales(k_scale_listed, K_LOADED, k_scale, K_SCALE_START)

        k_pool = []

        def load_first_keys(o, tag):
            k_pool.append(held([P, TOKENS], U32, "k_pool%d" % o, tag))
            nc.sync.dma_start(k_pool[o][:].bitcast(I32), k_words[o].rearrange("p t b -> p (t b)").bitcast(I32))


        c_listed = held([P, SLOTS], U32, "c_listed")
        nc.vector.tensor_copy(c_listed[:], c_pool[:].indirect(offsets[:]))
        c_codes = held([P, PASSES, 2 * SLOTS], U8, "c_codes")
        nc.vector.tensor_copy(c_codes[:].bitcast(U16), c_listed[:].bitcast(U16).rearrange("p (n h) -> p h n", h=PASSES))
        load_first_keys(0, "first_pool")

        th_turned = bank([P, P], "th_turned", 1)
        nc.tensor.transpose(th_turned[:], th_rows[:], identity[:])
        minus_th = held([P, CHUNKS], F32, "minus_th")
        nc.vector.tensor_scalar(out=minus_th[:], in0=th_turned[:, 0:CHUNKS], scalar1=-1.0, scalar2=None, op0=ALU.mult)

        q_codes = {}
        q_scale = {}
        q_rounded = {}

        def round_queries(o, pair, raw, copy):
            q_rounded[o, pair] = held([P, PAIR, PACK], BF16, "q_rounded%d%d" % (o, pair))
            copy(
                q_rounded[o, pair][:].rearrange("p (c i) t -> p c t i", i=LINE),
                raw[:, :, pair * PAIR : (pair + 1) * PAIR].rearrange("p t (c i) -> p c t i", i=LINE),
            )

        def quantize_queries(o, pair):
            codes = held([P, PAIR], U32, "q_codes%d%d" % (o, pair))
            scale = held([P, PAIR], U8, "q_scale%d%d" % (o, pair))
            nc.vector.quantize_mx(
                out=codes[:].bitcast(FP8X4), scales=scale[:], in_=q_rounded[o, pair][:].rearrange("p w t -> p (w t)")
            )
            for c in range(2):
                q_codes[o, 2 * pair + c] = codes[:, c * P : (c + 1) * P]
                q_scale[o, 2 * pair + c] = scale[:, c * P : (c + 1) * P]

        def scores(sums, j, o, codes, scale):
            nc.tensor.matmul_mx(
                out=sums[:],
                lhsT=q_codes[o, j].bitcast(FP8X4),
                lhsT_scale=q_scale[o, j],
                rhs=codes,
                rhs_scale=scale,
                start=(o == 0),
                stop=(o == PASSES - 1),
            )

        round_queries(0, 1, q_first, nc.scalar.copy)
        round_queries(0, 0, q_first, nc.vector.tensor_copy)
        quantize_queries(0, 0)
        quantize_queries(0, 1)
        load_first_keys(1, "first_queries")
        round_queries(1, 1, q_second, nc.vector.tensor_copy)
        round_queries(1, 0, q_second, nc.scalar.copy)
        quantize_queries(1, 1)

        z_bank_numbers = (3, 7, 4, 5)
        k_codes = [held([P, SLOTS], U32, "k_codes%d" % o) for o in range(PASSES)]
        z_banks = {}
        z_dealt = {}

        def second_scores(j, o):
            if o == 0:
                z_banks[j] = bank([P, SLOTS], "z_bank", z_bank_numbers[j])
            scores(z_banks[j], j, o, c_codes[:, o, :].bitcast(FP4X4), c_scale[:, o, :])

        def first_scores(j, o, parts=slice(None)):
            for first_slot, slots, part in a_parts[j][parts]:
                cols = slice(first_slot, first_slot + slots)
                scores(part, j, o, k_codes[o][:, cols].bitcast(FP8X4), k_scale[K_SCALE_START:P, o, cols])

        def deal_second_scores(j):
            z_dealt[j] = held([P, PACK, P], F32, "z_dealt%d" % j)
            nc.scalar.activation(
                out=z_dealt[j][:],
                in_=z_banks[j][:].rearrange("p (s r) -> p r s", r=PACK),
                func=ACT.Sigmoid if j == LAST_CHUNK else ACT.Identity,
                bias=minus_th[:, j : j + 1],
            )

        def turn(dealt, number):
            turned = bank([P, PACK, P], "turned", number)
            for r in range(PACK):
                nc.tensor.transpose(turned[:, r, :], dealt[:, r, :], identity[:])
            return turned

        for j in (0, 1, LAST_CHUNK, 2):
            second_scores(j, 0)
        quantize_queries(1, 0)
        for j in (LAST_CHUNK, 2):
            second_scores(j, 1)
            deal_second_scores(j)
        z_weights = held([P, PACK, P], F32, "z_weights")
        z_turned = turn(z_dealt[LAST_CHUNK], 6)
        for j in range(2):
            second_scores(j, 1)
            deal_second_scores(j)
        nc.scalar.copy(z_weights[:], z_turned[:])
        halves = {0: (0, 1), 1: (2, 3), LAST_CHUNK: (5, 7)}
        a_parts = {j: [(h * HALF, HALF, bank([P, HALF], "a_half", n)) for h, n in enumerate(halves[j])] for j in halves}
        a_parts[2] = [(0, SLOTS, bank([P, SLOTS], "a_bank", 4))]
        nc.vector.tensor_copy(k_codes[0][:], k_pool[0][:].indirect(offsets[:]))
        first_scores(0, 0)
        first_scores(1, 0, slice(0, 1))
        first_scores(LAST_CHUNK, 0, slice(0, 1))
        first_scores(2, 0)
        first_scores(1, 0, slice(1, 2))
        first_scores(LAST_CHUNK, 0, slice(1, 2))
        a_weights = held([P, PACK, P], F32, "a_weights")
        for h in range(2):
            listed = offsets[:, h * HALF // LIST_ROWS : (h + 1) * HALF // LIST_ROWS]
            nc.vector.tensor_copy(k_codes[1][:, h * HALF : (h + 1) * HALF], k_pool[1][:].indirect(listed))
            for j in halves:
                first_scores(j, 1, slice(h, h + 1))
            nc.scalar.activation(
                out=a_weights[:, :, h * HALF // PACK : (h + 1) * HALF // PACK],
                in_=a_parts[LAST_CHUNK][h][2][:].rearrange("p (s r) -> p r s", r=PACK),
                func=ACT.Sigmoid,
                bias=minus_th[:, LAST_CHUNK : LAST_CHUNK + 1],
            )
        first_scores(2, 1)

        y_codes = held([P, QUERIES], U32, "y_codes")
        y_scale = held([P, QUERIES], U8, "y_scale")
        y_rows = out_0.rearrange("(p r) q -> p r q", r=PACK)
        word_rows = out_1[0].rearrange("p q b -> p (q b)").bitcast(I32)
        last_pair = held([P, PACK, PAIR], F32, "last_pair")
        first_pair = held([P, PACK, PAIR], F32, "first_pair")
        weights2, weights3 = last_pair[:, :, 0:P], last_pair[:, :, P:PAIR]

        y_chunks = {0: 2, 2: 1, LAST_CHUNK: 1}
        best = [held([P, PACK, P], F32, "best%d" % j) for j in range(LAST_CHUNK)]

        def take_best(j, which, places):
            first_slot, slots, part = a_parts[j][which]
            rows = slice(first_slot // PACK, (first_slot + slots) // PACK)
            nc.vector.scalar_tensor_tensor(
                out=best[j][:, places, rows],
                in0=part[:].rearrange("p (s r) -> p r s", r=PACK)[:, places, :],
                scalar=minus_th[:, j : j + 1],
                in1=z_dealt[j][:, places, rows],
                op0=ALU.add,
                op1=ALU.max,
            )

        def weigh_first_pair(place, number):
            turned = bank([P, PAIR], "turned_pair", number)
            for j in range(2):
                nc.tensor.transpose(turned[:, j * P : (j + 1) * P], best[j][:, place, :], identity[:])
            nc.scalar.activation(out=first_pair[:, place, :], in_=turned[:], func=ACT.Sigmoid)
            nc.sync.dma_start(y_rows[:, place, 0:PAIR], first_pair[:, place, :])

        def weigh_chunk_2(place, number):
            places = slice(place, place + 2)
            take_best(2, 0, places)
            turned = bank([P, 2, P], "turned_places", number)
            for r in range(2):
                nc.tensor.transpose(turned[:, r, :], best[2][:, place + r, :], identity[:])
            nc.scalar.activation(out=weights2[:, places, :], in_=turned[:], func=ACT.Sigmoid)

        def round_weights(j, weights, copy):
            copy(
                y_rounded[j][:].rearrange("p (c i) r -> p c r i", i=LINE),
                weights.rearrange("p r (c i) -> p c r i", i=LINE),
            )

        def hand_on(j):
            cols = slice(j * P, (j + y_chunks[j]) * P)
            nc.vector.quantize_mx(
                out=y_codes[:, cols].bitcast(FP8X4),
                scales=y_scale[:, cols],
                in_=y_rounded[j][:].rearrange("p q r -> p (q r)"),
            )

        for j in range(2):
            take_best(j, 0, slice(0, PACK))
        for places in (slice(0, 1), slice(1, 2), slice(2, PACK)):
            for j in range(2):
                take_best(j, 1, places)
        for place, number in enumerate((6, 5, 0, 2)):
            weigh_first_pair(place, number)
        a_turned = turn(a_weights, 1)
        weigh_chunk_2(0, 7)
        weigh_chunk_2(2, 3)
        nc.vector.tensor_tensor(out=weights3, in0=a_turned[:], in1=z_weights[:], op=ALU.max)
        for place in (0, 2):
            nc.sync.dma_start(y_rows[:, place : place + 2, PAIR:QUERIES], last_pair[:, place : place + 2, :])

        y_tags = {0: "a_weights", 2: None, LAST_CHUNK: "best2"}
        y_rounded = {j: held([P, y_chunks[j] * P, PACK], BF16, "y_rounded%d" % j, y_tags[j]) for j in y_chunks}
        round_weights(LAST_CHUNK, weights3, nc.scalar.copy)
        round_weights(0, first_pair[:], nc.vector.tensor_copy)
        round_weights(2, weights2, nc.vector.tensor_copy)
        hand_on(0)
        nc.sync.dma_start(word_rows[:, 0:PAIR], y_codes[:, 0:PAIR].bitcast(I32))
        for j in (LAST_CHUNK, 2):
            hand_on(j)
        nc.sync.dma_start(word_rows[:, PAIR:QUERIES], y_codes[:, PAIR:QUERIES].bitcast(I32))
        for quad in range(QUADRANTS):
            (nc.scalar, nc.sync)[quad % 2].dma_start(
                out_2[0, SCALE_ROWS * quad : SCALE_ROWS * (quad + 1), :].bitcast(I32),
                y_scale[QUADRANT * quad : QUADRANT * quad + SCALE_ROWS, :].bitcast(I32),
            )
